import numpy as np, ml_dtypes
CORES = [16,18,20,22]
N = 4
import mx_ref
BF = ml_dtypes.bfloat16
def gcols(t, e):
    v = np.concatenate([t.reshape(8, 16, -1, 4), np.zeros((8, 16, 1, 4), BF)], axis=2)
    return np.ascontiguousarray(np.stack([v[g][:, e[g]] for g in range(8)])).reshape(128, -1)
def tile(rs):
    return np.stack(rs, axis=2).reshape(128, -1).astype(BF)
def pick(q, e):
    c = np.concatenate([q[0].reshape(128, -1, 4), np.zeros((128, 1, 4), np.uint8)], axis=1); s = np.concatenate([q[1], np.ones((16, 1), np.uint8)], axis=1)
    return (np.ascontiguousarray(c[:, e].reshape(128, -1)), np.ascontiguousarray(s[:, e]))
def join(*qs):
    return (np.concatenate([q[0] for q in qs], axis=1), np.concatenate([q[1] for q in qs], axis=1))
def put(q, e, v):
    c, s = q[0].reshape(128, -1, 4).copy(), q[1].copy(); c[:, e] = v[0].reshape(128, -1, 4); s[:, e] = v[1]
    return (c.reshape(128, -1), s)
def pk(c, s):
    return (np.ascontiguousarray(c), mx_ref.live(s))
def emit(q):
    return q[0], q[1]
def packed(v, rng):
    q = [mx_ref.quantize(np.ascontiguousarray(v[r])) for r in range(N)]
    return np.stack([a for a, b in q]), np.stack([mx_ref.plane(b, rng) for a, b in q])
def values_of_codes():
    e, c = np.zeros((128, 128, 4), np.float32), np.zeros((128, 2, 4), np.uint8)
    e[np.arange(128), np.arange(128), 0] = 1
    c[:127, :, 0] = np.arange(256).reshape(2, 128).T[:127]
    return mx_ref.matmul(mx_ref.quantize(e.reshape(128, 512).astype(BF)), (c.reshape(128, 8), np.full((16, 2), 127, np.uint8))).T.reshape(-1).astype(np.float64)
CODE_VALUE, SCALE_VALUE = values_of_codes(), 2.0 ** (np.arange(256) - 127.0)
def decode(q):
    return (CODE_VALUE[q[0]].reshape(16, 8, -1, 4) * SCALE_VALUE[q[1]][:, None, :, None] + 0.0).reshape(128, -1).astype(np.float32)
def f(rng, *shape):
    return mx_ref.flush((rng.standard_normal(shape, dtype=np.float32) * np.exp2(rng.integers(-2, 3, shape[:-1] + (1,)))).astype(BF))
def wide(rng, *shape, cols=0):
    v = rng.standard_normal(shape, dtype=np.float32) * np.exp2(rng.integers(-12, 13, shape)).astype(np.float32)
    if cols: v *= np.repeat(np.exp2(rng.integers(-cols, cols + 1, shape[:-2] + (1, shape[-1] // 4))) * (rng.random(shape[:-2] + (1, shape[-1] // 4)) > 0.0625), 4, axis=-1).astype(np.float32)
    return mx_ref.flush(v.astype(BF))
C, E = 448, 12
def big(v):
    v = v.astype(np.float32)
    v[np.abs(v) < np.float32(2.0 ** -16)] = 0
    return v.astype(BF)
def numbers_of(rng):
    return big(f(rng, N, 128, 4 * C)), big(f(rng, N, 128, 128)), np.array(f(rng, N, 128, 512)), np.array(f(rng, N, 128, 512))
def layers(rng):
    return big(f(rng, N, 128, 2048)).reshape(N, 8, 16, 4, 8, 16, 4)
def some(rng, k):
    return np.argsort(np.argsort(rng.random((8, 32)), axis=1), axis=1) < k
def flags(rng):
    k = np.where(some(rng, E // 2), -1.0, rng.random((N, 8, 32)))
    fl = np.ones((N, 8, 32), np.int32)
    np.put_along_axis(fl, np.argsort(k, axis=2)[:, :, :E], 0, axis=2)
    return fl
def relabels(rng):
    return np.argsort(rng.random((N, 7, 32, 32)), axis=3)
def drawn(rng, x, tr, u, v, fl, w, ti=None):
    t = tr.astype(np.float32).reshape(N, 8, 16, 32, 4).copy()
    t[np.broadcast_to((fl == 0)[:, :, None, :, None], t.shape)] = 0
    if ti is None: ti = relabels(rng)
    c, p = packed(np.ascontiguousarray(w).reshape(N, 128, 2048), rng)
    return {"x": np.ascontiguousarray(x).reshape(N, 128, 4 * C).astype(BF), "tr": t.reshape(N, 128, 128).astype(BF), "u": np.ascontiguousarray(u).reshape(N, 128, 512), "v": v, "fl": fl, "ti": ti.reshape(N, 7, 1024).astype(np.int32), "wc": c, "ws": p}
def setup_inputs(rng):
    x, tr, u, v = numbers_of(rng)
    return drawn(rng, x, tr, u, v, flags(rng), layers(rng))
def setup_inputs_ties(rng):
    x, tr, u, v = numbers_of(rng)
    o = rng.permutation(N)
    x = x.reshape(N, 8, 16, C, 4)
    for r in range(N):
        a = x[r][:, :8, :24].copy()
        a[:, :, 23] = 0
        k = rng.permutation(C) % 24
        if r == o[0]: k = np.zeros(C, int)
        if r == o[1]: k = np.full(C, 23)
        x[r][:, :8] = a[:, :, k]
    u = u.reshape(N, 8, 16, 128, 4)
    for i in range(5): u[:, :, 8:, i::16] = 0
    w = layers(rng)
    w[:, :, :, :, :, :8] = 0
    return drawn(rng, x, tr, u, v, flags(rng), w)
def setup_inputs_near(rng):
    x, tr, u, v = numbers_of(rng)
    fl, ti = flags(rng), relabels(rng)
    a = int(rng.integers(N))
    fl[(a + 1) % N] = fl[a]
    o = rng.permutation(N) % 2
    x = x.astype(np.float32).reshape(N, 8, 16, C, 4)
    tr = tr.astype(np.float32).reshape(N, 8, 16, 32, 4)
    x[:, :, :8] = 0
    tr[:, :, :8] = 0
    u = u.reshape(N, 128, 128, 4)
    for i in range(5): u[:, :, i::16] = 0
    for r in range(N):
        k = 2.0 ** -30 if o[r] == 0 else 1.0
        x[r, :, :5, :, 0] = k * rng.integers(-1, 2, (8, 5, C))
        tr[r, :, :5, :, 0] = k * rng.integers(-1, 2, (8, 5, 32))
        for g in rng.permutation(8)[:4]: x[r, g, :5, rng.integers(C), 0] = 2.0 ** 27 * rng.choice([-1.0, 1.0], 5)
        for h in range(0, 128, 16):
            for i in range(5): u[r, h + i, h + i, 0] = k
    hole = np.stack([np.flatnonzero(fl[a, g] == 0) for g in range(8)])
    held = np.stack([np.flatnonzero(fl[a, g] == 1) for g in range(8)])
    n = np.arange(8 * E)
    b = held[np.arange(8)[:, None], rng.integers(0, 32 - E, (8, 8 * E))]
    b[n // E, n] = hole[n // E, n % E]
    back = np.argsort(ti[a], axis=2)
    e = b.copy()
    for g in range(8):
        for h in range(g - 1, -1, -1): e[g] = back[h, b[h], e[g]]
    bit = (e[:, None] >> np.arange(4, -1, -1)[:, None]) & 1
    j = rng.permutation(C)[:8 * E]
    s = x[a, :, :5, :, 0]
    m = np.abs(s[:, :, j])
    s[:, :, j] = np.where(bit == 1, np.maximum(m, 2.0 ** -30 if o[a] == 0 else 1.0), 0.0 - m)
    x[a, :, :5, :, 0] = s
    w = layers(rng)
    w[:, :, :8] = 0
    w[:, :, :, :, :, :8] = 0
    return drawn(rng, x, tr, u, v, fl, w, ti)
def setup_inputs_deep(rng):
    x, tr, u, v = numbers_of(rng)
    x = (rng.integers(0, 2, x.shape) * 2.0 - 1.0) * (0.8 + 0.2 * rng.random(x.shape)) * 2.0 ** 26
    tr = (rng.integers(0, 2, tr.shape) * 2.0 - 1.0) * (0.8 + 0.2 * rng.random(tr.shape)) * 2.0 ** 26
    u = (rng.integers(0, 2, u.shape) * 2.0 - 1.0) * (0.9 + 0.1 * rng.random(u.shape)) * 2.0 ** 30
    o = rng.permutation(N)
    m = some(rng, E)
    fl = np.ones((N, 8, 32), np.int32)
    for r in range(N):
        if r == o[1]: fl[r, 7][m[7]] = 0
        elif r == o[2]: fl[r, 0][m[0]] = 0
        elif r != o[0]: fl[r][m] = 0
    w = (layers(rng).astype(np.float32) * np.float32(0.0625)).astype(BF)
    return drawn(rng, x.astype(np.float32), tr.astype(np.float32), u.astype(np.float32).astype(BF), v, fl, w)
def setup_inputs_odd(rng):
    x, tr, u, v = numbers_of(rng)
    x = (1.125 + 0.25 * rng.integers(0, 4, (N, 16, 8, C, 4))) * np.exp2(-rng.integers(8, 15, (N, 16, 8, C, 4)).astype(np.float32))
    x[:, :, 0, :, 0] = 1.96875
    x = x * (rng.integers(0, 2, x.shape) * 2.0 - 1.0) * np.exp2(rng.integers(-2, 3, (N, 16, 1, C, 1)).astype(np.float32))
    return drawn(rng, x.astype(np.float32), tr, u, v, flags(rng), layers(rng))
def setup_inputs_spread(rng):
    x, tr, u, v = numbers_of(rng)
    return drawn(rng, big(wide(rng, N, 128, 4 * C, cols=6)), big(wide(rng, N, 128, 128)), u, v, flags(rng), layers(rng))
def check_inputs(d):
    b = []
    for k in ("x", "tr", "u", "v"):
        a = np.abs(d[k].astype(np.float32))
        if not (np.isfinite(a).all() and ((a == 0) | (a >= 2.0 ** -30) & (a <= 2.0 ** 30)).all()): b.append("a value of " + k)
    fl = d["fl"]
    if not ((fl == 0) | (fl == 1)).all(): b.append("a flag of fl")
    if (np.sum(fl == 0, axis=2) > E).any(): b.append("too many empty slots in a level")
    if ((d["tr"].astype(np.float32).reshape(N, 8, 16, 32, 4) != 0) & (fl == 0)[:, :, None, :, None]).any(): b.append("tr isn't zero at an empty slot")
    if (np.sort(d["ti"].reshape(N, 7, 32, 32), axis=3) != np.arange(32)).any(): b.append("ti: not the points in some order")
    none, least, most = [emit(mx_ref.quantize(np.full((128, 16), k, np.float32).astype(BF)))[1][0, 0] for k in (0.0, 2.0 ** -30, 2.0 ** 30)]
    for r in range(N):
        if ((d["wc"][r] == 0x7F) | (d["wc"][r] == 0xFF)).any(): b.append("wc: a code that is no number")
        s = mx_ref.live(d["ws"][r])
        if ((s != none) & ((s < least) | (s > most))).any(): b.append("ws: a scale out of range")
    return b
def reference(x, tr, u, v, fl, ti, wc, ws):
    qu = [mx_ref.quantize(u[r]) for r in range(N)]
    lay = [pk(wc[r], ws[r]) for r in range(N)]
    now = [x[r] for r in range(N)]
    slot = [decode(mx_ref.quantize(tr[r])).astype(BF) for r in range(N)]
    full = fl > 0
    way = np.zeros((N, 8, C), np.int64)
    for t in range(3):
        claim, came = [], []
        for r in range(N):
            q = mx_ref.quantize(now[r])
            own = decode(q)
            s = mx_ref.matmul(qu[r], q)
            e = 16 * (s[0::16] > 0) + 8 * (s[1::16] > 0) + 4 * (s[2::16] > 0) + 2 * (s[3::16] > 0) + (s[4::16] > 0)
            fail = np.full(C, 8)
            for g in range(8):
                going = fail == 8
                way[r, g] = np.where(going, e[g], -1)
                fail = np.where(going & ~full[r, g][e[g]], g, fail)
                if g < 7: e[g + 1:] = ti[r, g][32 * e[g] + e[g + 1:]]
            passed = np.where(np.arange(8)[:, None] < fail, way[r], -1)
            z = (own - gcols(slot[r], passed).astype(np.float32)).astype(BF)
            q = mx_ref.quantize(z)
            c = np.full((8, 32), C)
            j = np.flatnonzero(fail < 8)
            np.minimum.at(c, (fail[j], way[r][fail[j], j]), j)
            claim.append(c < C)
            came.append(gcols(decode(q).astype(BF), np.where(c < C, c, -1)))
            now[r] = tile([mx_ref.matmul(pick(lay[r], np.arange(128 * b, 128 * b + 128)), q) * np.float32(0.015625) + z[:, b::4].astype(np.float32) for b in range(4)])
        for r in range(N):
            take = claim[(r - 1) % N] & ~full[r]
            slot[r] = gcols(np.concatenate([slot[r], came[(r - 1) % N]], axis=1), np.arange(32) + 32 * take)
            full[r] = full[r] | take
    y, bp, rt = np.zeros((N, 128, C), np.float32), np.zeros((N, 8, C + 32), np.float32), np.zeros((N, 128, 128), np.float32)
    oc, osc = np.zeros((N, 128, 4 * C), np.uint8), np.zeros((N, 16, C), np.uint8)
    for r in range(N):
        q = mx_ref.quantize(now[r])
        y[r] = mx_ref.matmul(mx_ref.quantize(v[r]), q)
        bp[r] = np.concatenate([way[r], full[r]], axis=1)
        rt[r] = slot[r].astype(np.float32)
        oc[r], osc[r] = emit(q)
    return {"y": y, "bp": bp, "rt": rt, "oc": oc, "osc": osc}

@@ -1,0 +1,542 @@
+from concourse.mybir import dt, AluOpType, ActivationFunctionType
+
+ROUNDS = 3
+H = 224
+NS = 2
+WIN = 2144
+PEN0, ID0 = 1120, 1136
+OCC = 32.0 * (PEN0 - 32)
+ZW = 464
+COPY = ActivationFunctionType.Copy
+AO = AluOpType
+
+SCRATCH = {
+    "ub": ("sbuf", [128, 512], "bfloat16"), "uq": ("sbuf", [128, 128], "float8_e4m3fn_x4"), "us": ("sbuf", [128, 128], "uint8"),
+    "vb": ("sbuf", [128, 512], "bfloat16"), "vq": ("sbuf", [128, 128], "float8_e4m3fn_x4"), "vs": ("sbuf", [128, 128], "uint8"),
+    "wq": ("sbuf", [128, 512], "float8_e4m3fn_x4"), "wp": ("sbuf", [128, 512], "uint8"),
+    "ec": ("sbuf", [128, 2048], "bfloat16"), "em": ("sbuf", [128, 2048], "bfloat16"),
+    "eq": ("sbuf", [128, 512], "float8_e4m3fn_x4"), "es": ("sbuf", [128, 512], "uint8"),
+    "tb": ("sbuf", [128, 512], "bfloat16"), "tq": ("sbuf", [128, 128], "float8_e4m3fn_x4"), "tsc": ("sbuf", [128, 128], "uint8"),
+    "zt": ("sbuf", [128, 512], "bfloat16"),
+    "tii": ("sbuf", [128, 64], "int32"), "tif": ("sbuf", [128, 64], "bfloat16"), "td": ("dram", [16, 7168], "bfloat16"),
+    "tab": ("sbuf", [128, 7 * WIN], "bfloat16"),
+    "rowi": ("sbuf", [128, 256], "int32"), "row": ("sbuf", [128, 256], "float32"), "flb": ("sbuf", [128, 256], "float32"),
+    "idv": ("sbuf", [128, 32], "float32"), "pi": ("sbuf", [128, 1], "int32"), "pj": ("sbuf", [128, 1], "int32"),
+    "k2": ("sbuf", [128, 2], "float32"), "ix": ("sbuf", [128, 48], "float32"), "bw": ("sbuf", [128, 48], "float32"),
+    "d0": ("sbuf", [128, 96], "float32"), "dg": ("sbuf", [128, 96], "bfloat16"),
+    "bs": ("sbuf", [128, 2], "float32"), "dd": ("sbuf", [128, 2], "float32"), "k4": ("sbuf", [128, 4], "float32"),
+    "cf": ("sbuf", [128, 320], "bfloat16"), "ones": ("sbuf", [128, H], "bfloat16"),
+    "oi": ("sbuf", [128, 2], "int32"),
+    "nt": ("sbuf", [128, 192], "bfloat16"),
+    "zp": ("sbuf", [128, 4 * ZW], "bfloat16"),
+    "ct": ("sbuf", [128, 512], "bfloat16"),
+    "na": ("sbuf", [128, 2], "float32"), "nn": ("sbuf", [128, 2], "float32"), "jo": ("sbuf", [128, 2], "uint16"),
+    "thr": ("sbuf", [128, 2], "float32"), "tk": ("sbuf", [128, 2], "float32"), "tm": ("sbuf", [128, 2], "float32"),
+    "sr": ("sbuf", [128, 2], "float32"), "mo": ("sbuf", [128, 8], "uint16"),
+    "rto": ("sbuf", [128, 128], "float32"), "ys": ("sbuf", [128, 448], "float32"),
+}
+for _s in range(NS):
+    for _n, _w, _d in (("xb", 4 * H, "bfloat16"), ("zb", 4 * H, "bfloat16"), ("nf", 4 * H, "bfloat16"),
+                       ("xq", H, "float8_e4m3fn_x4"), ("xs", H, "uint8"), ("zq", H, "float8_e4m3fn_x4"), ("zs", H, "uint8"),
+                       ("bt", 320, "bfloat16"), ("sc", 320, "bfloat16"), ("go", 640, "bfloat16"), ("tr7", 8 * 320, "bfloat16"),
+                       ("of", 40, "uint16"), ("va", 16, "bfloat16"), ("vd", 16, "bfloat16"),
+                       ("lb", 16, "bfloat16"), ("lu", 14, "uint16"), ("qe", 2 * H, "bfloat16"), ("sn", 2 * H, "bfloat16"),
+                       ("bo", H, "float32")):
+        SCRATCH[_n + str(_s)] = ("sbuf", [128, _w], _d)
+for _r in range(ROUNDS + 1):
+    SCRATCH["oc%d" % _r] = ("sbuf", [128, 2], "float32")
+    SCRATCH["tw%d" % _r] = ("sbuf", [128, 256], "bfloat16")
+for _r in range(ROUNDS):
+    SCRATCH["as%d" % _r] = ("sbuf", [128, 2], "float32")
+    SCRATCH["al%d" % _r] = ("sbuf", [128, 2], "float32")
+    SCRATCH["cq%d" % _r] = ("sbuf", [128, 128], "float8_e4m3fn_x4")
+    SCRATCH["cs%d" % _r] = ("sbuf", [128, 128], "uint8")
+    SCRATCH["lq%d" % _r] = ("sbuf", [128, 160], "float8_e4m3fn_x4")
+    SCRATCH["ls%d" % _r] = ("sbuf", [128, 160], "uint8")
+for _b in range(8):
+    SCRATCH["ps%d" % _b] = ("psum", [128, 512], "float32")
+
+DMA_SEMS = (["x0", "x1", "lu_", "lw", "lv", "ltr", "lti", "lfl", "lrow", "tdw", "out"] + ["tb%d" % i for i in range(7)]
+            + ["l%d%d" % (s, r) for s in range(NS) for r in range(ROUNDS)] + ["fr%d" % r for r in range(ROUNDS)])
+SEMAPHORES = (["qV", "qS", "qT", "qG", "loc"] + ["d_" + n for n in DMA_SEMS]
+              + ["aa%d" % r for r in range(ROUNDS)] + ["ac%d" % r for r in range(ROUNDS)])
+NE = 8
+
+CY = 0.00083
+WAKE = 0.09
+SLACK = 0.03
+BIAS = 0.4
+AHEAD = 0.5
+
+
+def vw(name, c0=0, c1=None, st=1, p0=0, p1=128, ps=1):
+    if c1 is None:
+        c1 = SCRATCH[name][1][1]
+    return (name, c0, c1, st, p0, p1, ps)
+
+
+def width(a):
+    return len(range(a[1], a[2], a[3]))
+
+
+def AP(T, a):
+    n, c0, c1, st, p0, p1, ps = a
+    rows = slice(p0, p1) if ps == 1 else slice(p0, p1, ps)
+    cols = slice(c0, c1) if st == 1 else slice(c0, c1, st)
+    return T[n][rows, cols]
+
+
+def overlap(a, b):
+    if a[0][:2] == "ps" and a[0] == b[0]:
+        return True
+    if a[1] >= b[2] or b[1] >= a[2] or a[4] >= b[5] or b[4] >= a[5]:
+        return False
+    if a[3] == b[3] and a[3] > 1 and (a[1] - b[1]) % a[3]:
+        return False
+    return True
+
+
+def plan():
+    ops = []
+
+    def add(q, fn, R, W, dur, sem=None, inc=1, lat=0.0, pri=0.0, kind="c"):
+        ops.append({"q": q, "fn": fn, "R": R, "W": W, "dur": dur, "sem": sem or "q" + q, "inc": inc, "lat": lat, "pri": pri, "kind": kind})
+
+    def two(*v):
+        return all(SCRATCH[a[0]][2] in ("bfloat16", "uint16") for a in v)
+
+    def memset(o, val):
+        add("V", lambda T, g, o=o, val=val: g.vector.memset(AP(T, o), val), [], [o], 0.055 + width(o) * CY * (0.5 if two(o) else 1))
+
+    def tt(o, a, b, op, ind=None, pri=0.0):
+        def fn(T, g):
+            i0 = AP(T, a)
+            if ind is not None:
+                i0 = i0.indirect(AP(T, ind))
+            return g.vector.tensor_tensor(AP(T, o), i0, AP(T, b), op)
+        f = 1.56 if ind is not None else (1.0 if "ps" in (a[0][:2], b[0][:2]) else 2.0)
+        add("V", fn, [a, b] + ([ind] if ind is not None else []), [o], 0.055 + width(o) * CY * f, pri=pri)
+
+    def ts(o, a, s1, op0, s2=None, op1=None, pri=0.0):
+        def fn(T, g):
+            x1 = AP(T, s1) if isinstance(s1, tuple) else s1
+            x2 = AP(T, s2) if isinstance(s2, tuple) else s2
+            if op1 is None:
+                return g.vector.tensor_scalar(AP(T, o), AP(T, a), x1, None, op0)
+            return g.vector.tensor_scalar(AP(T, o), AP(T, a), x1, x2, op0, op1)
+        add("V", fn, [a] + [s for s in (s1, s2) if isinstance(s, tuple)], [o], 0.055 + width(o) * CY, pri=pri)
+
+    def vcopy(o, a):
+        add("V", lambda T, g: g.vector.tensor_copy(AP(T, o), AP(T, a)), [a], [o], 0.055 + width(o) * CY)
+
+    def scan(o, a, b, init, op0, op1, pri=0.0):
+        add("V", lambda T, g: g.vector.tensor_tensor_scan(AP(T, o), AP(T, a), AP(T, b), init, op0, op1), [a, b], [o], 0.055 + width(o) * CY * 0.5, pri=pri)
+
+    def flip(o, a):
+        add("V", lambda T, g: g.vector.transpose(AP(T, o), AP(T, a)), [a], [o], 0.055 + width(o) * CY * 0.5)
+
+    def quant(o, s, a):
+        add("V", lambda T, g: g.vector.quantize_mx(AP(T, o), AP(T, s), AP(T, a)), [a], [o, s], 0.02 + width(a) * 0.00022)
+
+    def act(o, a, scale=None, ind=None, pri=0.0):
+        def src(T):
+            i = AP(T, a)
+            return i if ind is None else i.indirect(AP(T, ind))
+
+        def fs(T, g):
+            if scale is None:
+                return g.scalar.activation(AP(T, o), src(T), COPY)
+            return g.scalar.activation(AP(T, o), src(T), COPY, scale=scale)
+
+        def fv(T, g):
+            if scale is None:
+                return g.vector.tensor_copy(AP(T, o), src(T))
+            return g.vector.tensor_scalar(AP(T, o), src(T), scale, None, AO.mult)
+        f = 1.56 if ind is not None else 1.0
+        add("S", fs, [a] + ([ind] if ind is not None else []), [o], 0.065 + width(o) * CY * f, pri=pri)
+        ops[-1]["alt"] = ("V", fv, 0.055 + width(o) * CY * (0.5 if ind is None and two(a, o) else f))
+
+    def mm(o, l, ls, m, ms):
+        add("T", lambda T, g: g.tensor.matmul_mx(AP(T, o), AP(T, l), AP(T, ls), AP(T, m), AP(T, ms), True, True),
+            [l, ls, m, ms], [o], 0.03 + (width(m) + 16) * 0.00075)
+
+    def dma(q, sem, o, i, R, W, size=0, pri=0.0):
+        fy = lambda T, g: g.sync.dma_start(o(T), i(T))
+        fs = lambda T, g: g.scalar.dma_start(o(T), i(T))
+        add(q[0], fy if q[0] == "Y" else fs, R, W, 0.07, sem="d_" + sem, inc=16, lat=1.9 + size / 200000.0, pri=pri, kind="d")
+        if q == "YS":
+            ops[-1]["alt"] = ("S", fs, 0.07)
+
+    for s in range(NS):
+        dma("Y", "x%d" % s, lambda T, s=s: T["xb%d" % s][:], lambda T, s=s: T.x[:, 4 * H * s:4 * H * (s + 1)], [], [vw("xb%d" % s)], 230000, pri=50)
+    dma("S", "lu_", lambda T: T.ub[:], lambda T: T.u[:], [], [vw("ub")], 130000, pri=50)
+    dma("S", "lti", lambda T: T.tii[0:112, :], lambda T: T.ti[:], [], [vw("tii", p1=112)], 28000, pri=60)
+    dma("S", "lrow", lambda T: T.rowi[0:1, :], lambda T: T.fl[:], [], [vw("rowi", p1=1)], pri=45)
+    dma("S", "lfl", lambda T: T.oi[:], lambda T: T.fl[:], [], [vw("oi")], pri=10)
+    dma("Y", "ltr", lambda T: T.tb[:, 0:128], lambda T: T.tr[:], [], [vw("tb", 0, 128)], 30000, pri=30)
+    ts(vw("tif", p1=112), vw("tii", p1=112), 32.0, AO.mult, 32.0, AO.add, pri=60)
+    for m in range(16):
+        dma("YS"[m % 2], "tdw", lambda T, m=m: T.td[m:m + 1, :], lambda T: T.tif[0:112, :], [vw("tif", p1=112)], [("td", 0, 7168, 1, m, m + 1, 1)], 14000, pri=55)
+    for gl in range(7):
+        o = WIN * gl
+        lo = 0 if gl == 0 else 33
+        a = o + lo
+        if lo:
+            memset(vw("tab", o, a), 0.0)
+        if gl in (2, 4, 6):
+            memset(vw("tab", o + ID0 - 32, o + ID0 - 31), 0.0)
+        for m in range(8):
+            dma("Y", "tb%d" % gl, lambda T, m=m, a=a: T.tab[16 * m:16 * m + 16, a:a + 1024], lambda T, gl=gl: T.td[:, 1024 * gl:1024 * gl + 1024],
+                [("td", 1024 * gl, 1024 * gl + 1024, 1, 0, 16, 1)], [vw("tab", a - a % 8, a + 1024 + (-a) % 8, p0=16 * m, p1=16 * m + 16)], 32000, pri=40 - 2 * gl)
+    dma("Y", "lw", lambda T: T.wq[:].bitcast(dt.uint8), lambda T: T.wc[:], [], [vw("wq")], 260000)
+    dma("Y", "lw", lambda T: T.wp[:], lambda T: T.ws[:], [], [vw("wp")], 65000)
+    dma("Y", "lv", lambda T: T.vb[:], lambda T: T.v[:], [], [vw("vb")], 130000, pri=-20)
+
+    def iota(o, pat, base, cm, flag):
+        def fn(T, g):
+            if flag:
+                return g.iota(AP(T, o), pat, base, cm, allow_small_or_imprecise_dtypes=True)
+            return g.iota(AP(T, o), pat, base, cm)
+        add("G", fn, [], [o], 0.13 + 2 * width(o) * CY)
+    memset(vw("em"), -0.015625)
+    for h in range(2):
+        v = vw("ec", 1024 * h, 1024 * h + 1024)
+        iv = vw("em", 1024 * h, 1024 * h + 1024)
+        add("G", lambda T, g, v=v, iv=iv, h=h: g.affine_select(AP(T, v), AP(T, iv), [[-1, 2], [1, 512]], AO.is_equal, 0.0, -2 * h, -4), [iv], [v], 0.17 + 2048 * CY)
+        quant(vw("eq", 256 * h, 256 * h + 256), vw("es", 256 * h, 256 * h + 256), v)
+    iota(vw("idv"), [[32, 32]], 32, 0, True)
+    iota(vw("pi"), [[0, 1]], 0, 1, False)
+    iota(vw("ix"), [[1, 48]], 0, 0, True)
+    iota(vw("bw"), [[1, 48]], -1, 0, True)
+    iota(vw("k4"), [[32, 4]], 0, 0, True)
+    ts(vw("pj"), vw("pi"), 15, AO.bitwise_and)
+    for c in range(2):
+        ts(vw("k2", c, c + 1), vw("pj"), 2.0, AO.mult, 1.0 + c, AO.add)
+        ts(vw("d0", 48 * c, 48 * c + 48), vw("ix"), vw("k2", c, c + 1), AO.not_equal, -448.0, AO.mult)
+        ts(vw("bs", c, c + 1), vw("pj"), 2.0, AO.mult, float(c), AO.add)
+        ts(vw("dd", c, c + 1), vw("pj"), -1.0, AO.mult, 128.0 + 15 * c, AO.add)
+    ts(vw("dg"), vw("d0"), -224.0, AO.add)
+    memset(vw("cf"), 2.0)
+    memset(vw("cf", 0, 320, 16), 0.0)
+    for s in range(NS):
+        memset(vw("cf", 160 * s + 128, 160 * s + 160), 0.0)
+        for b in range(2):
+            memset(vw("bt%d" % s, 160 * b + 128, 160 * b + 144), 32.0 * PEN0)
+            memset(vw("bt%d" % s, 160 * b + 144, 160 * b + 160), 32.0 * ID0)
+        for gl in (2, 4, 6):
+            c = 320 * gl + 32 * (9 - gl)
+            memset(vw("tr7%d" % s, c, c + 32), 32.0 * (ID0 - 32))
+    memset(vw("ones"), 1.0)
+    memset(vw("nt"), 0.0)
+    for t in range(4):
+        memset(vw("zp", ZW * t + 448, ZW * t + ZW), 0.0)
+    memset(vw("tb", 128, 512), 0.0)
+    memset(vw("zt"), 0.0)
+    memset(vw("ct"), 0.0)
+    for gl in (0, 2, 4, 6):
+        act(vw("tab", WIN * gl + ID0, WIN * gl + ID0 + 993, 32), vw("idv"))
+    for r in range(ROUNDS):
+        quant(vw("lq%d" % r, 32, 160), vw("ls%d" % r, 32, 160), vw("zt"))
+    quant(vw("uq"), vw("us"), vw("ub"))
+    vcopy(vw("row", p1=1), vw("rowi", p1=1))
+    vcopy(vw("oc0"), vw("oi"))
+
+    def flags_out():
+        for a, b in ((0, 64), (64, 224)):
+            add("G", lambda T, g, a=a, b=b: g.partition_broadcast(T.flb[:, a:b], T.row[0:1, a:b], 128), [vw("row", a, b, p1=1)], [vw("flb", a, b)], 0.14 + 4 * (b - a) * CY, pri=10)
+        for gl in range(7):
+            act(vw("tab", WIN * gl + PEN0, WIN * gl + PEN0 + 993, 32), vw("flb", 32 * gl, 32 * gl + 32), OCC)
+    flags_out()
+
+    def scores(s):
+        for b in range(2):
+            p = vw("ps%d" % (4 * s + b), 0, 128)
+            mm(p, vw("xq%d" % s, 96 * b, 96 * b + 128), vw("xs%d" % s, 96 * b, 96 * b + 128), vw("uq"), vw("us"))
+            ts(vw("bt%d" % s, 160 * b, 160 * b + 128), p, 0.0, AO.is_gt, 32.0, AO.mult)
+        scan(vw("sc%d" % s), vw("cf"), vw("bt%d" % s), 0.0, AO.mult, AO.add)
+
+    def unpack(s):
+        for t in range(4):
+            p = vw("ps%d" % (4 * s + (2, 3, 0, 1)[t]), 0, H)
+            mm(p, vw("eq", 128 * t, 128 * t + 128), vw("es", 128 * t, 128 * t + 128), vw("xq%d" % s), vw("xs%d" % s))
+            act(vw("nf%d" % s, H * t, H * t + H), p)
+
+    for s in range(NS):
+        quant(vw("xq%d" % s), vw("xs%d" % s), vw("xb%d" % s))
+        scores(s)
+    for s in range(NS):
+        unpack(s)
+    quant(vw("tq"), vw("tsc"), vw("tb"))
+    for t in range(4):
+        p = vw("ps%d" % t, 0, 128)
+        mm(p, vw("eq", 128 * t, 128 * t + 128), vw("es", 128 * t, 128 * t + 128), vw("tq"), vw("tsc"))
+        act(vw("tw0", 32 * t, 32 * t + 32), vw("ps%d" % t, 0, 32))
+        act(vw("nt", 48 * t + 1, 48 * t + 33), vw("tw0", 32 * t, 32 * t + 32))
+    quant(vw("vq"), vw("vs"), vw("vb"))
+
+    def level(s, gl, r):
+        nh = 7 - gl
+        runs = nh + 1 + (gl % 2 == 0)
+        tr, va, of, go = "tr7%d" % s, "va%d" % s, "of%d" % s, "go%d" % s
+        fo, fg = 20 * (gl % 2), 320 * (gl % 2)
+        base = 320 * gl
+        for k in range(2):
+            if gl == 0:
+                i0 = vw("sc%d" % s, 160 * k + 20, 160 * k + 149, 16)
+                b = vw("sc%d" % s, 160 * k + 4, 160 * k + 5)
+            else:
+                i0 = vw(tr, base + 32 + 16 * k, base + 32 * runs + 16 * k + 1, 32)
+                b = vw(va, 2 * gl + k, 2 * gl + k + 1)
+            ts(vw(of, fo + k, fo + 2 * runs - 1 + k, 2), i0, 0.03125, AO.mult, b, AO.add)
+        act(vw(go, fg, fg + 32 * runs), vw("tab", WIN * gl, WIN * gl + WIN), None, vw(of, fo, fo + 2 * runs))
+        n = base + 320
+        flip(vw(tr, n, n + 32 * runs), vw(go, fg, fg + 32 * runs))
+        g1 = gl + 1
+        tt(vw(va, 2 * g1, 2 * g1 + 2), vw(tr, n, n + 17, 16), vw(tr, n + 32 * nh, n + 32 * nh + 17, 16), AO.min)
+        if g1 % 2:
+            act(vw("vd%d" % s, 2 * gl, 2 * gl + 2), vw(tr, n + 32 * (nh + 1), n + 32 * (nh + 1) + 17, 16))
+            for lv, buf in ((gl, "vd%d" % s), (g1, va)):
+                for a in range(4):
+                    for h in range(2):
+                        if a == 0 and h == 1:
+                            continue
+                        p0, c0 = 32 * a + 16 * h, 6 * h + 2 * a
+                        dma("YS" if gl == 6 else "Y", "l%d%d" % (s, r), lambda T, lv=lv, c0=c0: T["lb%d" % s][16 * lv:16 * lv + 16, c0:c0 + 2],
+                            lambda T, lv=lv, p0=p0, buf=buf: T[buf][p0:p0 + 16, 2 * lv:2 * lv + 2],
+                            [vw(buf, 2 * lv, 2 * lv + 2, p0=p0, p1=p0 + 16)], [vw("lb%d" % s, c0, c0 + 2, p0=16 * lv, p1=16 * lv + 16)], pri=20 if gl == 6 else 0)
+
+    for r in range(ROUNDS):
+        last = r == ROUNDS - 1
+        for gl in range(7):
+            for s in range(NS):
+                n0 = len(ops)
+                level(s, gl, r)
+                for o in ops[n0:]:
+                    o["pri"] += AHEAD * (1 - s)
+        for s in range(NS):
+            lu = vw("lu%d" % s)
+            ts(lu, vw("lb%d" % s, 0, 14), 0.03125, AO.mult, pri=3)
+            for c in range(2):
+                e = vw("qe%d" % s, H * c, H * c + H)
+                act(e, vw("dg", 48 * c, 48 * c + 48), None, lu, pri=6)
+                scan(vw("sn%d" % s, H * c, H * c + H), e, vw("ones"), -672.0, AO.max, AO.add, pri=6)
+        ts(vw("thr"), vw("oc%d" % r), 1224.0, AO.mult, -224.0, AO.add)
+        ts(vw("na"), vw("sn0", H - 1, 2 * H, H), 224.0, AO.add, pri=6)
+        tt(vw("nn"), vw("na"), vw("sn1", H - 1, 2 * H, H), AO.max, pri=6)
+        tt(vw("as%d" % r), vw("nn"), vw("thr"), AO.is_gt, pri=6)
+        ts(vw("jo"), vw("nn"), -1.0, AO.mult, 224.0, AO.add, pri=3)
+        remote(add, "as%d" % r, "al%d" % r, 2, "aa%d" % r)
+        if last:
+            for s in range(NS):
+                act(vw("bo%d" % s), vw("bw"), None, vw("lu%d" % s))
+                dma("Y", "out", lambda T, s=s: T.bp[:, H * s:H * s + H], lambda T, s=s: T["bo%d" % s][0:128:16, :], [vw("bo%d" % s)], [])
+        for s in range(NS):
+            for t in range(4):
+                z = vw("zb%d" % s, t, 4 * H, 4)
+                tt(z, vw("nt", 48 * t, 48 * t + 48), vw("nf%d" % s, H * t, H * t + H), AO.subtract, ind=vw("lu%d" % s))
+                act(vw("zp", ZW * t + H * s, ZW * t + H * s + H), z, 64.0)
+            quant(vw("zq%d" % s), vw("zs%d" % s), vw("zb%d" % s))
+        for t in range(4):
+            act(vw("ct", t, 128, 4), vw("zp", ZW * t, ZW * t + ZW), None, vw("jo"), pri=1)
+        quant(vw("cq%d" % r), vw("cs%d" % r), vw("ct"))
+        remote(add, "cq%d" % r, "lq%d" % r, 32, "ac%d" % r)
+        remote(add, "cs%d" % r, "ls%d" % r, 32, "ac%d" % r)
+        for s in range(NS):
+            for k in range(4):
+                p = vw("ps%d" % (4 * s + k), 0, H)
+                mm(p, vw("wq", 128 * k, 128 * k + 128), vw("wp", 128 * k, 128 * k + 128), vw("zq%d" % s), vw("zs%d" % s))
+                tt(vw("xb%d" % s, k, 4 * H, 4), p, vw("zp", ZW * k + H * s, ZW * k + H * s + H), AO.add)
+            quant(vw("xq%d" % s), vw("xs%d" % s), vw("xb%d" % s))
+            if not last:
+                scores(s)
+        add("", None, [vw("as%d" % r)], [vw("al%d" % r)], 0.0, sem="aa%d" % r, inc=NE, lat=1.8, kind="a")
+        tt(vw("oc%d" % (r + 1)), vw("oc%d" % r), vw("al%d" % r), AO.max, pri=6)
+        dma("Y", "fr%d" % r, (lambda T: T.bp[:, 448:480]) if last else (lambda T: T.row[0:1, :]), lambda T, r=r: T["oc%d" % (r + 1)][:],
+            [vw("oc%d" % (r + 1))], [] if last else [vw("row", p1=1)], pri=6)
+        if not last:
+            flags_out()
+            for s in range(NS):
+                unpack(s)
+        else:
+            for s in range(NS):
+                p = vw("ps%d" % (4 * s), 0, H)
+                mm(p, vw("vq"), vw("vs"), vw("xq%d" % s), vw("xs%d" % s))
+                act(vw("ys", H * s, H * s + H), p)
+                dma("Y", "out", lambda T, s=s: T.y[:, H * s:H * s + H], lambda T, s=s: T.ys[:, H * s:H * s + H], [vw("ys", H * s, H * s + H)], [], 115000)
+                dma("Y", "out", lambda T, s=s: T.oc[:, 4 * H * s:4 * H * (s + 1)], lambda T, s=s: T["xq%d" % s][:].bitcast(dt.uint8), [vw("xq%d" % s)], [], 115000)
+                for k in range(4):
+                    dma("Y", "out", lambda T, s=s, k=k: T.osc[4 * k:4 * k + 4, H * s:H * s + H], lambda T, s=s, k=k: T["xs%d" % s][32 * k:32 * k + 4, :],
+                        [vw("xs%d" % s)], [])
+        add("", None, [vw("cq%d" % r), vw("cs%d" % r)], [vw("lq%d" % r, 0, 32), vw("ls%d" % r, 0, 32)], 0.0, sem="ac%d" % r, inc=2 * NE, lat=2.2, kind="a")
+        tt(vw("tk"), vw("al%d" % r), vw("oc%d" % r), AO.is_gt)
+        tt(vw("tm"), vw("tk"), vw("dd"), AO.mult)
+        tt(vw("sr"), vw("tm"), vw("bs"), AO.add)
+        for t in range(4):
+            p = 4 + t if last else t
+            mm(vw("ps%d" % p, 0, 128), vw("eq", 128 * t, 128 * t + 128), vw("es", 128 * t, 128 * t + 128), vw("lq%d" % r, 0, 128), vw("ls%d" % r, 0, 128))
+            act(vw("tw%d" % r, 128 + 32 * t, 160 + 32 * t), vw("ps%d" % p, 0, 32))
+        for c in range(2):
+            ts(vw("mo", 4 * c, 4 * c + 4), vw("k4"), vw("sr", c, c + 1), AO.add)
+            act(vw("tw%d" % (r + 1), c, 128, 2), vw("tw%d" % r), None, vw("mo", 4 * c, 4 * c + 4))
+        for t in range(4):
+            if last:
+                act(vw("rto", t, 128, 4), vw("tw%d" % (r + 1), 32 * t, 32 * t + 32), -64.0)
+            else:
+                act(vw("nt", 48 * t + 1, 48 * t + 33), vw("tw%d" % (r + 1), 32 * t, 32 * t + 32))
+    dma("Y", "out", lambda T: T.rt[:], lambda T: T.rto[:], [vw("rto")], [], 65000)
+    return ops
+
+
+def remote(add, src, dst, n, sem):
+    code = SCRATCH[src][2].startswith("float8")
+
+    def fn(T, g, topo, core, to):
+        a, b = T[dst][:, 0:n], T[src][:, 0:n]
+        if code:
+            a, b = a.bitcast(dt.uint8), b.bitcast(dt.uint8)
+        rid, pid = topo.addr(to)[0], topo.addr(to)[1]
+        m = 0
+        for e in topo.engines(core, to)[:NE]:
+            m |= 1 << e
+        return g.remote_dma(a, b, T.sem[sem], T.sem.loc, pid, rid, m)
+    add("G", fn, [vw(src, 0, n)], [], 0.3, sem="loc", inc=NE, lat=0.0, kind="r", pri=6)
+
+
+def schedule(ops):
+    n = len(ops)
+    deps = [set() for _ in range(n)]
+    acc, groups = {}, {}
+    for i, o in enumerate(ops):
+        if o["kind"] == "d":
+            groups.setdefault(o["sem"], []).append(i)
+    for i, o in enumerate(ops):
+        for v, w in [(a, False) for a in o["R"]] + [(a, True) for a in o["W"]]:
+            for j, u, uw in acc.setdefault(v[0], []):
+                if j == i or j in deps[i]:
+                    continue
+                bank = v[0][:2] == "ps" and (ops[j]["q"] != o["q"] or "alt" in o or "alt" in ops[j])
+                if (w or uw or bank) and overlap(u, v):
+                    deps[i].add(j)
+        for v, w in [(a, False) for a in o["R"]] + [(a, True) for a in o["W"]]:
+            lst = acc[v[0]]
+            if w:
+                lst[:] = [t for t in lst if not (v[3] == 1 and v[6] == 1 and t[1][1] >= v[1] and t[1][2] <= v[2] and t[1][4] >= v[4] and t[1][5] <= v[5]) or t[0] == i]
+            lst.append((i, v, w))
+    for i in range(n):
+        for j in list(deps[i]):
+            if ops[j]["kind"] == "d":
+                for m in groups[ops[j]["sem"]]:
+                    assert m < i
+                    deps[i].add(m)
+    for i, o in enumerate(ops):
+        if o["kind"] == "a":
+            for j in range(i):
+                if ops[j]["kind"] == "r" and any(a[0] == b[0] for a in ops[j]["R"] for b in o["R"]):
+                    deps[i].add(j)
+    succ = [[] for _ in range(n)]
+    for i in range(n):
+        for j in deps[i]:
+            succ[j].append(i)
+    pri = [0.0] * n
+    for i in range(n - 1, -1, -1):
+        o = ops[i]
+        pri[i] = o["dur"] + o["lat"] + max([pri[k] + WAKE for k in succ[i]], default=0.0)
+    left = [len(d) for d in deps]
+    done, free, order, est = [0.0] * n, {}, [], {}
+    for i in range(n):
+        if not left[i]:
+            est[i] = 0.0
+
+    def ways(i):
+        o = ops[i]
+        r = []
+        for q, fn, dur in [(o["q"], o["fn"], o["dur"])] + ([o["alt"]] if "alt" in o else []):
+            t = max(est[i], free.get(q, 0.0)) if q else est[i]
+            r.append((t + dur, t, q, fn, dur))
+        return min(r, key=lambda x: x[0] + (BIAS if len(r) > 1 and x[2] == "V" else 0.0))
+    while est:
+        W = {i: ways(i) for i in est}
+        best = min(est, key=lambda i: (W[i][1], -pri[i] - ops[i]["pri"]))
+        t0 = W[best][1]
+        cand = [i for i in est if W[i][2] == W[best][2] and W[i][1] <= t0 + SLACK]
+        i = max(cand, key=lambda i: (pri[i] + ops[i]["pri"], -i))
+        end, t, q, fn, dur = W[i]
+        if "alt" in ops[i]:
+            ops[i].update({"q": q, "fn": fn, "dur": dur})
+            if ops[i]["kind"] == "c":
+                ops[i]["sem"] = "q" + q
+        if q:
+            free[q] = end
+        done[i] = end + ops[i]["lat"]
+        order.append((t, i))
+        del est[i]
+        for k in succ[i]:
+            left[k] -= 1
+            if not left[k]:
+                est[k] = max(done[j] for j in deps[k]) + WAKE
+    return [i for _, i in order], deps, done, order
+
+
+_CACHE = {}
+
+
+def rank_program(g, core, T, topo):
+    rank = T.rank_of(core)
+    if rank is None:
+        return
+    if not _CACHE:
+        _CACHE["ops"] = plan()
+        _CACHE["order"] = schedule(_CACHE["ops"])
+    ops = _CACHE["ops"]
+    order, deps, _, _ = _CACHE["order"]
+    to = T.cores[(rank + 1) % len(T.cores)]
+    queue = {"V": g.vector, "S": g.scalar, "T": g.tensor, "G": g, "Y": g.sync}
+    total, count, known, clock = {}, {}, {}, {}
+    for o in ops:
+        if o["kind"] == "d":
+            total[o["sem"]] = total.get(o["sem"], 0) + o["inc"]
+
+    def need(j):
+        o = ops[j]
+        return (o["sem"], total[o["sem"]] if o["kind"] == "d" else o["inc"] if o["kind"] == "a" else count[j])
+
+    for i in order:
+        o = ops[i]
+        q = o["q"]
+        if o["kind"] == "a":
+            clock[i] = {o["sem"]: o["inc"]}
+            continue
+        k = known.setdefault(q, {})
+        want = {}
+        for j in sorted(deps[i], reverse=True):
+            sem, c = need(j)
+            if k.get(sem, 0) < c and want.get(sem, (0, 0))[0] < c:
+                want[sem] = (c, j)
+        for sem in sorted(want, key=lambda s: -want[s][1]):
+            c, j = want[sem]
+            if k.get(sem, 0) >= c:
+                continue
+            queue[q].wait_ge(T.sem[sem], c)
+            for s2, c2 in clock[j].items():
+                if k.get(s2, 0) < c2:
+                    k[s2] = c2
+            if k.get(sem, 0) < c:
+                k[sem] = c
+        if o["kind"] == "r":
+            o["fn"](T, g, topo, core, to)
+            total["loc"] = total.get("loc", 0) + o["inc"]
+            clock[i] = {}
+            continue
+        o["fn"](T, g).then_inc(T.sem[o["sem"]], o["inc"])
+        clock[i] = dict(k)
+        if o["kind"] == "d":
+            clock[i][o["sem"]] = total[o["sem"]]
+        else:
+            total[o["sem"]] = total.get(o["sem"], 0) + 1
+            count[i] = total[o["sem"]]
+            clock[i][o["sem"]] = count[i]
+    for r in range(ROUNDS):
+        g.wait_ge(T.sem["aa%d" % r], NE)
+        g.wait_ge(T.sem["ac%d" % r], 2 * NE)
+    for sem in total:
+        g.wait_ge(T.sem[sem], total[sem])

@@ -7,6 +7,8 @@ WIN = 2144
 PEN0, ID0 = 1120, 1136
 OCC = 32.0 * (PEN0 - 32)
 ZW = 464
+ZS = (3,)
+NE = 8
 COPY = ActivationFunctionType.Copy
 AO = AluOpType
 
@@ -19,30 +21,27 @@ SCRATCH = {
     "tb": ("sbuf", [128, 512], "bfloat16"), "tq": ("sbuf", [128, 128], "float8_e4m3fn_x4"), "tsc": ("sbuf", [128, 128], "uint8"),
     "zt": ("sbuf", [128, 512], "bfloat16"),
     "tii": ("sbuf", [128, 64], "int32"), "tif": ("sbuf", [128, 64], "bfloat16"), "td": ("dram", [16, 7168], "bfloat16"),
-    "tab": ("sbuf", [128, 7 * WIN], "bfloat16"),
+    "t0d": ("dram", [16, 1024], "int32"), "t0": ("sbuf", [128, WIN], "int32"), "tab": ("sbuf", [128, 7 * WIN], "bfloat16"),
     "rowi": ("sbuf", [128, 256], "int32"), "row": ("sbuf", [128, 256], "float32"), "flb": ("sbuf", [128, 256], "float32"),
     "idv": ("sbuf", [128, 32], "float32"), "pi": ("sbuf", [128, 1], "int32"), "pj": ("sbuf", [128, 1], "int32"),
-    "k2": ("sbuf", [128, 2], "float32"), "ix": ("sbuf", [128, 48], "float32"), "bw": ("sbuf", [128, 48], "float32"),
-    "d0": ("sbuf", [128, 96], "float32"), "dg": ("sbuf", [128, 96], "bfloat16"),
-    "bs": ("sbuf", [128, 2], "float32"), "dd": ("sbuf", [128, 2], "float32"), "k4": ("sbuf", [128, 4], "float32"),
-    "cf": ("sbuf", [128, 320], "bfloat16"), "ones": ("sbuf", [128, H], "bfloat16"),
-    "oi": ("sbuf", [128, 2], "int32"),
-    "nt": ("sbuf", [128, 192], "bfloat16"),
-    "zp": ("sbuf", [128, 4 * ZW], "bfloat16"),
-    "ct": ("sbuf", [128, 512], "bfloat16"),
+    "k2": ("sbuf", [128, 2], "float32"), "ix": ("sbuf", [128, 96], "float32"),
+    "d0": ("sbuf", [128, 96], "float32"), "dg": ("sbuf", [128, 96], "bfloat16"), "kc": ("sbuf", [128, 8], "float32"),
+    "cf": ("sbuf", [128, 100], "bfloat16"), "ones": ("sbuf", [128, H], "bfloat16"), "oi": ("sbuf", [128, 2], "int32"),
+    "nt": ("sbuf", [128, 192], "bfloat16"), "zp": ("sbuf", [128, 4 * ZW], "bfloat16"), "ct": ("sbuf", [128, 512], "bfloat16"),
     "na": ("sbuf", [128, 2], "float32"), "nn": ("sbuf", [128, 2], "float32"), "jo": ("sbuf", [128, 2], "uint16"),
     "thr": ("sbuf", [128, 2], "float32"), "tk": ("sbuf", [128, 2], "float32"), "tm": ("sbuf", [128, 2], "float32"),
     "sr": ("sbuf", [128, 2], "float32"), "mo": ("sbuf", [128, 8], "uint16"),
     "rto": ("sbuf", [128, 128], "float32"), "ys": ("sbuf", [128, 448], "float32"),
 }
 for _s in range(NS):
-    for _n, _w, _d in (("xb", 4 * H, "bfloat16"), ("zb", 4 * H, "bfloat16"), ("nf", 4 * H, "bfloat16"),
+    for _n, _w, _d in (("xb", 4 * H, "bfloat16"), ("zb", 4 * H, "bfloat16"), ("nf", 4 * H, "bfloat16"), ("tg", 4 * H, "bfloat16"),
                        ("xq", H, "float8_e4m3fn_x4"), ("xs", H, "uint8"), ("zq", H, "float8_e4m3fn_x4"), ("zs", H, "uint8"),
-                       ("bt", 320, "bfloat16"), ("sc", 320, "bfloat16"), ("go", 640, "bfloat16"), ("tr7", 8 * 320, "bfloat16"),
-                       ("of", 40, "uint16"), ("va", 16, "bfloat16"), ("vd", 16, "bfloat16"),
+                       ("bt", 100, "bfloat16"), ("sc", 100, "bfloat16"), ("go", 640, "bfloat16"), ("tr7", 8 * 320, "bfloat16"),
+                       ("of", 40, "uint16"), ("va", 16, "bfloat16"), ("vp", 16, "bfloat16"), ("cb", 8, "bfloat16"),
                        ("lb", 16, "bfloat16"), ("lu", 14, "uint16"), ("qe", 2 * H, "bfloat16"), ("sn", 2 * H, "bfloat16"),
                        ("bo", H, "float32")):
         SCRATCH[_n + str(_s)] = ("sbuf", [128, _w], _d)
+    SCRATCH["md" + str(_s)] = ("dram", [16, 7, 16], "bfloat16")
 for _r in range(ROUNDS + 1):
     SCRATCH["oc%d" % _r] = ("sbuf", [128, 2], "float32")
     SCRATCH["tw%d" % _r] = ("sbuf", [128, 256], "bfloat16")
@@ -56,17 +55,24 @@ for _r in range(ROUNDS):
 for _b in range(8):
     SCRATCH["ps%d" % _b] = ("psum", [128, 512], "float32")
 
-DMA_SEMS = (["x0", "x1", "lu_", "lw", "lv", "ltr", "lti", "lfl", "lrow", "tdw", "out"] + ["tb%d" % i for i in range(7)]
-            + ["l%d%d" % (s, r) for s in range(NS) for r in range(ROUNDS)] + ["fr%d" % r for r in range(ROUNDS)])
+DMA_SEMS = (["x0", "x1", "lu_", "lw", "lv", "ltr", "lti", "lfl", "lrow", "tdw", "t0d", "t0", "out"] + ["tb%d" % i for i in range(7)]
+            + [k + "%d%d" % (s, r) for k in "lm" for s in range(NS) for r in range(ROUNDS)] + ["fr%d" % r for r in range(ROUNDS)])
 SEMAPHORES = (["qV", "qS", "qT", "qG", "loc"] + ["d_" + n for n in DMA_SEMS]
               + ["aa%d" % r for r in range(ROUNDS)] + ["ac%d" % r for r in range(ROUNDS)])
-NE = 8
 
 CY = 0.00083
 WAKE = 0.09
-SLACK = 0.03
-BIAS = 0.4
-AHEAD = 0.5
+SLACK = 0.05
+BIAS = 0.6
+AHEAD = 5
+PRI = {'go': 9.0, 'ps': 13.5, 'nn': 26.0, 'zb': 18.5, 'sn': 42.0, 'tw': -16.0, 'flb': 12.0, 'xq': 15.0, 'uq': 30.5, 'nt': -7.5, 'va': 26.0, 'rto': -18.0, 'bod': -6.0,
+       'tq': 21.5, 'tm': 1.5, 'as': 5.0, 'xbd': -20.0, 'mdd': -14.5, 'ec': 12.5, 'ys': -8.5, 'cqd': 14.5, 'xqd': 2.5, 'tabd': 13.5, 'csd': 11.5, 'jo': -1.0,
+       'vq': -14.5, 'ix': -14.0, 'sc': 5.5, 'mo': -40, 'cb': -16.5, 'rowid': -9.0, 'zt': 2.5, 'em': 5.5, 'tif': -10.5, 'tab': 1.5, 'row': -1.5, 'ones': -4.0,
+       'thr': 8.0, 'wpd': -11.0, 'xsd': -59.5, 't': -9.5, 'na': 4.0, 'rtod': -3.0, 'oc': -6.5, 'sr': 8.0, 'vp': 2.0, 'pi': -15.0, 'tbd': 6.0, 'lbd': -16.5, 'asd': 5.0,
+       'vbd': 24.5, 't0dd': 2.5, 'td': -1.0, 'idv': 13.5, 'qe': 0.5, 'tb': 1.5, 'cf': 33.5, 'lq': 13.0, 'rowd': 19.5, 'tdd': 7.5, 'tg': 0.5, 'tk': -6.0, 'd': -2.5,
+       'oid': 19.5, 'dg': 28.5, 'lu': 3.0, 'ubd': -7.5, 'nf': -12.0, 'ocd': 11.5, 'tiid': -6.5, 'ysd': -3.0, 'bo': -8.0, 'pj': -1.0, 'wqd': 6.5, 'k': 2, 'bt': -1,
+       'zp': -0.5, 'zq': 1, 'kc': -8.0, 'eq': -1, 'xb': 0.5, 'ct': 1}
+BIASES = {'nf': 3, 'zp': 0.1, 'go': 3, 'qe': 0.1, 'tab': 0.4, 'tw': 0, 'ys': 0.1, 'nt': 0.2, 'rto': 0.1, 'bo': 0.2, 'vp': 0, 'tg': 0.4, 'ct': 3}
 
 
 def vw(name, c0=0, c1=None, st=1, p0=0, p1=128, ps=1):
@@ -169,25 +175,32 @@ def plan():
 
     for s in range(NS):
         dma("Y", "x%d" % s, lambda T, s=s: T["xb%d" % s][:], lambda T, s=s: T.x[:, 4 * H * s:4 * H * (s + 1)], [], [vw("xb%d" % s)], 230000, pri=50)
-    dma("S", "lu_", lambda T: T.ub[:], lambda T: T.u[:], [], [vw("ub")], 130000, pri=50)
     dma("S", "lti", lambda T: T.tii[0:112, :], lambda T: T.ti[:], [], [vw("tii", p1=112)], 28000, pri=60)
+    for gl in range(8):
+        dma("S", "lu_", lambda T, gl=gl: T.ub[:, 20 * gl:20 * gl + 20], lambda T, gl=gl: T.u[:, 64 * gl:64 * gl + 20], [], [vw("ub", 20 * gl, 20 * gl + 20)], 10000, pri=50)
+    dma("S", "lu_", lambda T: T.ub[:, 160:512], lambda T: T.u[:, 0:352], [], [vw("ub", 160, 512)], 90000, pri=50)
     dma("S", "lrow", lambda T: T.rowi[0:1, :], lambda T: T.fl[:], [], [vw("rowi", p1=1)], pri=45)
     dma("S", "lfl", lambda T: T.oi[:], lambda T: T.fl[:], [], [vw("oi")], pri=10)
     dma("Y", "ltr", lambda T: T.tb[:, 0:128], lambda T: T.tr[:], [], [vw("tb", 0, 128)], 30000, pri=30)
     ts(vw("tif", p1=112), vw("tii", p1=112), 32.0, AO.mult, 32.0, AO.add, pri=60)
     for m in range(16):
         dma("YS"[m % 2], "tdw", lambda T, m=m: T.td[m:m + 1, :], lambda T: T.tif[0:112, :], [vw("tif", p1=112)], [("td", 0, 7168, 1, m, m + 1, 1)], 14000, pri=55)
-    for gl in range(7):
+    for m in range(8):
+        dma("YS"[m % 2], "t0d", lambda T, m=m: T.t0d[m:m + 1, :], lambda T: T.ti[0:1, :], [], [("t0d", 0, 1024, 1, m, m + 1, 1)], 4000, pri=70)
+    for m in range(16):
+        dma("YS"[m % 2], "t0", lambda T, m=m: T.t0[8 * m:8 * m + 8, 0:1024], lambda T: T.t0d[0:8, :], [("t0d", 0, 1024, 1, 0, 8, 1)], [vw("t0", 0, 1024, p0=8 * m, p1=8 * m + 8)], 32000, pri=65)
+    for gl in (1, 2, 3, 4, 5, 6, 0):
         o = WIN * gl
-        lo = 0 if gl == 0 else 33
-        a = o + lo
-        if lo:
+        a = o + (0 if gl == 0 else 33)
+        if gl:
             memset(vw("tab", o, a), 0.0)
-        if gl in (2, 4, 6):
+        if gl in (4, 6):
             memset(vw("tab", o + ID0 - 32, o + ID0 - 31), 0.0)
+        if gl == 3:
+            memset(vw("tab", o + PEN0 - 32, o + PEN0 - 31), 0.0)
         for m in range(8):
-            dma("Y", "tb%d" % gl, lambda T, m=m, a=a: T.tab[16 * m:16 * m + 16, a:a + 1024], lambda T, gl=gl: T.td[:, 1024 * gl:1024 * gl + 1024],
-                [("td", 1024 * gl, 1024 * gl + 1024, 1, 0, 16, 1)], [vw("tab", a - a % 8, a + 1024 + (-a) % 8, p0=16 * m, p1=16 * m + 16)], 32000, pri=40 - 2 * gl)
+            dma("YS"[m % 2] if gl in (1, 2, 3) else "Y", "tb%d" % gl, lambda T, m=m, a=a: T.tab[16 * m:16 * m + 16, a:a + 1024], lambda T, gl=gl: T.td[:, 1024 * gl:1024 * gl + 1024],
+                [("td", 1024 * gl, 1024 * gl + 1024, 1, 0, 16, 1)], [vw("tab", a - a % 8, a + 1024 + (-a) % 8, p0=16 * m, p1=16 * m + 16)], 32000, pri=40 - 2 * (gl or 7))
     dma("Y", "lw", lambda T: T.wq[:].bitcast(dt.uint8), lambda T: T.wc[:], [], [vw("wq")], 260000)
     dma("Y", "lw", lambda T: T.wp[:], lambda T: T.ws[:], [], [vw("wp")], 65000)
     dma("Y", "lv", lambda T: T.vb[:], lambda T: T.v[:], [], [vw("vb")], 130000, pri=-20)
@@ -206,24 +219,23 @@ def plan():
         quant(vw("eq", 256 * h, 256 * h + 256), vw("es", 256 * h, 256 * h + 256), v)
     iota(vw("idv"), [[32, 32]], 32, 0, True)
     iota(vw("pi"), [[0, 1]], 0, 1, False)
-    iota(vw("ix"), [[1, 48]], 0, 0, True)
-    iota(vw("bw"), [[1, 48]], -1, 0, True)
-    iota(vw("k4"), [[32, 4]], 0, 0, True)
+    iota(vw("ix", 0, 48), [[1, 48]], 0, 0, True)
+    iota(vw("ix", 48, 96), [[1, 48]], -1, 0, True)
+    iota(vw("kc", 4, 8), [[32, 4]], 0, 0, True)
     ts(vw("pj"), vw("pi"), 15, AO.bitwise_and)
     for c in range(2):
         ts(vw("k2", c, c + 1), vw("pj"), 2.0, AO.mult, 1.0 + c, AO.add)
-        ts(vw("d0", 48 * c, 48 * c + 48), vw("ix"), vw("k2", c, c + 1), AO.not_equal, -448.0, AO.mult)
-        ts(vw("bs", c, c + 1), vw("pj"), 2.0, AO.mult, float(c), AO.add)
-        ts(vw("dd", c, c + 1), vw("pj"), -1.0, AO.mult, 128.0 + 15 * c, AO.add)
+        ts(vw("d0", 48 * c, 48 * c + 48), vw("ix", 0, 48), vw("k2", c, c + 1), AO.not_equal, -448.0, AO.mult)
+        ts(vw("kc", c, c + 1), vw("pj"), 2.0, AO.mult, float(c), AO.add)
+        ts(vw("kc", 2 + c, 3 + c), vw("pj"), -1.0, AO.mult, 128.0 + 15 * c, AO.add)
     ts(vw("dg"), vw("d0"), -224.0, AO.add)
     memset(vw("cf"), 2.0)
-    memset(vw("cf", 0, 320, 16), 0.0)
+    memset(vw("cf", 0, 100, 5), 0.0)
     for s in range(NS):
-        memset(vw("cf", 160 * s + 128, 160 * s + 160), 0.0)
+        memset(vw("cf", 50 * s + 40, 50 * s + 50), 0.0)
         for b in range(2):
-            memset(vw("bt%d" % s, 160 * b + 128, 160 * b + 144), 32.0 * PEN0)
-            memset(vw("bt%d" % s, 160 * b + 144, 160 * b + 160), 32.0 * ID0)
-        for gl in (2, 4, 6):
+            memset(vw("bt%d" % s, 50 * b + 40, 50 * b + 50), 32.0 * ID0)
+        for gl in (4, 6):
             c = 320 * gl + 32 * (9 - gl)
             memset(vw("tr7%d" % s, c, c + 32), 32.0 * (ID0 - 32))
     memset(vw("ones"), 1.0)
@@ -233,7 +245,7 @@ def plan():
     memset(vw("tb", 128, 512), 0.0)
     memset(vw("zt"), 0.0)
     memset(vw("ct"), 0.0)
-    for gl in (0, 2, 4, 6):
+    for gl in (0, 1, 2, 4, 6):
         act(vw("tab", WIN * gl + ID0, WIN * gl + ID0 + 993, 32), vw("idv"))
     for r in range(ROUNDS):
         quant(vw("lq%d" % r, 32, 160), vw("ls%d" % r, 32, 160), vw("zt"))
@@ -242,24 +254,26 @@ def plan():
     vcopy(vw("oc0"), vw("oi"))
 
     def flags_out():
-        for a, b in ((0, 64), (64, 224)):
+        for a, b in ((0, 96), (96, 224)):
             add("G", lambda T, g, a=a, b=b: g.partition_broadcast(T.flb[:, a:b], T.row[0:1, a:b], 128), [vw("row", a, b, p1=1)], [vw("flb", a, b)], 0.14 + 4 * (b - a) * CY, pri=10)
-        for gl in range(7):
-            act(vw("tab", WIN * gl + PEN0, WIN * gl + PEN0 + 993, 32), vw("flb", 32 * gl, 32 * gl + 32), OCC)
+        for gl, at in ((0, 2 * WIN + 4), (1, 2 * WIN + 8), (2, 2 * WIN), (3, 3 * WIN), (4, 4 * WIN), (5, 5 * WIN), (6, 6 * WIN)):
+            act(vw("tab", at + PEN0, at + PEN0 + 993, 32), vw("flb", 32 * gl, 32 * gl + 32), OCC)
     flags_out()
+    ts(vw("t0", ID0, ID0 + 993, 32), vw("idv"), 0.03125, AO.mult, -1.0, AO.add)
 
     def scores(s):
         for b in range(2):
             p = vw("ps%d" % (4 * s + b), 0, 128)
             mm(p, vw("xq%d" % s, 96 * b, 96 * b + 128), vw("xs%d" % s, 96 * b, 96 * b + 128), vw("uq"), vw("us"))
-            ts(vw("bt%d" % s, 160 * b, 160 * b + 128), p, 0.0, AO.is_gt, 32.0, AO.mult)
+            ts(vw("bt%d" % s, 50 * b, 50 * b + 40), vw("ps%d" % (4 * s + b), 0, 40), 0.0, AO.is_gt, 32.0, AO.mult)
         scan(vw("sc%d" % s), vw("cf"), vw("bt%d" % s), 0.0, AO.mult, AO.add)
 
     def unpack(s):
         for t in range(4):
             p = vw("ps%d" % (4 * s + (2, 3, 0, 1)[t]), 0, H)
             mm(p, vw("eq", 128 * t, 128 * t + 128), vw("es", 128 * t, 128 * t + 128), vw("xq%d" % s), vw("xs%d" % s))
-            act(vw("nf%d" % s, H * t, H * t + H), p)
+            if t not in ZS:
+                act(vw("nf%d" % s, H * t, H * t + H), p)
 
     for s in range(NS):
         quant(vw("xq%d" % s), vw("xs%d" % s), vw("xb%d" % s))
@@ -268,42 +282,76 @@ def plan():
         unpack(s)
     quant(vw("tq"), vw("tsc"), vw("tb"))
     for t in range(4):
-        p = vw("ps%d" % t, 0, 128)
-        mm(p, vw("eq", 128 * t, 128 * t + 128), vw("es", 128 * t, 128 * t + 128), vw("tq"), vw("tsc"))
-        act(vw("tw0", 32 * t, 32 * t + 32), vw("ps%d" % t, 0, 32))
+        pb = (2, 3, 6, 7)[t]
+        mm(vw("ps%d" % pb, 0, 128), vw("eq", 128 * t, 128 * t + 128), vw("es", 128 * t, 128 * t + 128), vw("tq"), vw("tsc"))
+        act(vw("tw0", 32 * t, 32 * t + 32), vw("ps%d" % pb, 0, 32))
         act(vw("nt", 48 * t + 1, 48 * t + 33), vw("tw0", 32 * t, 32 * t + 32))
     quant(vw("vq"), vw("vs"), vw("vb"))
 
     def level(s, gl, r):
-        nh = 7 - gl
-        runs = nh + 1 + (gl % 2 == 0)
-        tr, va, of, go = "tr7%d" % s, "va%d" % s, "of%d" % s, "go%d" % s
-        fo, fg = 20 * (gl % 2), 320 * (gl % 2)
-        base = 320 * gl
+        tr, va, vp, of, go, cb = ["%s%d" % (n, s) for n in ("tr7", "va", "vp", "of", "go", "cb")]
+        fo, fg, base = 20 * (gl % 2), 320 * (gl % 2), 320 * gl
+
+        def run(lv, k):
+            return vw(tr, 320 * lv + 32 * k, 320 * lv + 32 * k + 17, 16)
+        pre = 3 if gl == 2 else 0
+        nin = 7 - gl + (1, 0, 0, 0, 2, 1, 2)[gl]
+        pv = 4 if gl == 3 else 1
         for k in range(2):
             if gl == 0:
-                i0 = vw("sc%d" % s, 160 * k + 20, 160 * k + 149, 16)
-                b = vw("sc%d" % s, 160 * k + 4, 160 * k + 5)
+                i0, b = vw("sc%d" % s, 50 * k + 9, 50 * k + 45, 5), vw("sc%d" % s, 50 * k + 4, 50 * k + 5)
             else:
-                i0 = vw(tr, base + 32 + 16 * k, base + 32 * runs + 16 * k + 1, 32)
-                b = vw(va, 2 * gl + k, 2 * gl + k + 1)
-            ts(vw(of, fo + k, fo + 2 * runs - 1 + k, 2), i0, 0.03125, AO.mult, b, AO.add)
-        act(vw(go, fg, fg + 32 * runs), vw("tab", WIN * gl, WIN * gl + WIN), None, vw(of, fo, fo + 2 * runs))
+                i0 = vw(tr, base + 32 * pv + 16 * k, base + 32 * (pv + nin - 1) + 16 * k + 1, 32)
+                b = vw(tr, base + 16 * k, base + 16 * k + 1) if gl < 3 else vw(va if gl in (4, 6) else vp, 2 * gl + k, 2 * gl + k + 1)
+            ts(vw(of, fo + 2 * pre + k, fo + 2 * (pre + nin) - 1 + k, 2), i0, 0.03125, AO.mult, b, AO.add)
+        runs = pre + nin
+        if gl in (1, 2, 3):
+            ts(vw(of, fo + 2 * runs, fo + 2 * runs + 2), vw(vp, 6, 8) if gl == 3 else run(gl, 0), float((PEN0 if gl == 3 else ID0) - 32), AO.add)
+            runs += 1
+        if gl == 2:
+            ts(vw(of, fo, fo + 2), vw("sc%d" % s, 4, 55, 50), float(PEN0 + 4), AO.add)
+            ts(vw(of, fo + 2, fo + 4), run(2, 6), float(PEN0 + 8 - 32), AO.add)
+            ts(vw(of, fo + 4, fo + 6), run(2, 0), float(PEN0 - 32), AO.add)
+        if gl == 0 and r == 0:
+            add("V", lambda T, g: g.vector.tensor_scalar(T[go][:, 0:256], T.t0[:].indirect(T[of][:, 0:16]), 32.0, 32.0, AO.mult, AO.add),
+                [vw("t0"), vw(of, 0, 16)], [vw(go, 0, 256)], 0.055 + 256 * CY * 1.56)
+        else:
+            act(vw(go, fg, fg + 32 * runs), vw("tab", WIN * gl, WIN * gl + WIN), None, vw(of, fo, fo + 2 * runs))
         n = base + 320
         flip(vw(tr, n, n + 32 * runs), vw(go, fg, fg + 32 * runs))
         g1 = gl + 1
-        tt(vw(va, 2 * g1, 2 * g1 + 2), vw(tr, n, n + 17, 16), vw(tr, n + 32 * nh, n + 32 * nh + 17, 16), AO.min)
-        if g1 % 2:
-            act(vw("vd%d" % s, 2 * gl, 2 * gl + 2), vw(tr, n + 32 * (nh + 1), n + 32 * (nh + 1) + 17, 16))
-            for lv, buf in ((gl, "vd%d" % s), (g1, va)):
-                for a in range(4):
-                    for h in range(2):
-                        if a == 0 and h == 1:
-                            continue
-                        p0, c0 = 32 * a + 16 * h, 6 * h + 2 * a
-                        dma("YS" if gl == 6 else "Y", "l%d%d" % (s, r), lambda T, lv=lv, c0=c0: T["lb%d" % s][16 * lv:16 * lv + 16, c0:c0 + 2],
-                            lambda T, lv=lv, p0=p0, buf=buf: T[buf][p0:p0 + 16, 2 * lv:2 * lv + 2],
-                            [vw(buf, 2 * lv, 2 * lv + 2, p0=p0, p1=p0 + 16)], [vw("lb%d" % s, c0, c0 + 2, p0=16 * lv, p1=16 * lv + 16)], pri=20 if gl == 6 else 0)
+        blocks = [(32 * a, a) for a in range(4)] + [(32 * a + 16, a + 3) for a in range(1, 4)]
+        lbn, ls, md = "lb%d" % s, "l%d%d" % (s, r), "md%d" % s
+        if g1 == 1:
+            act(vw(vp, 0, 2), run(1, 7))
+        if g1 == 3:
+            for k in range(2):
+                v = vw(tr, n + 16 * k, n + 97 + 16 * k, 32)
+                scan(vw(cb, k, 7 + k, 2), v, v, 100000.0, AO.min, AO.min)
+            for lv, v, c in ((3, run(3, 3), 6), (1, run(1, 0), 0), (2, run(3, 8), 2)):
+                tt(vw(vp, 2 * lv, 2 * lv + 2), v, vw(cb, c, c + 2), AO.min)
+            for p0, c in blocks:
+                dma("YS", "m%d%d" % (s, r), lambda T, c=c: T[md][:, c, 0:8], lambda T, p0=p0: T[vp][p0:p0 + 16, 0:8],
+                    [vw(vp, 0, 8, p0=p0, p1=p0 + 16)], [(md, 16 * c, 16 * c + 16, 1, 0, 16, 1)], pri=10)
+            for lv in range(4):
+                dma("Y", ls, lambda T, lv=lv: T[lbn][16 * lv:16 * lv + 16, 0:14], lambda T, lv=lv: T[md][:, :, 2 * lv:2 * lv + 2],
+                    [(md, 0, 112, 1, 0, 16, 1)], [vw(lbn, 0, 14, p0=16 * lv, p1=16 * lv + 16)], pri=10)
+        if g1 == 4:
+            tt(vw(va, 8, 10), run(4, 0), run(4, 4), AO.min)
+        if g1 == 5:
+            tt(vw(vp, 10, 12), run(5, 0), run(5, 3), AO.min)
+            act(vw(vp, 8, 10), run(5, 4))
+        if g1 == 6:
+            tt(vw(va, 12, 14), run(6, 0), run(6, 2), AO.min)
+        if g1 == 7:
+            tt(vw(vp, 14, 16), run(7, 0), run(7, 1), AO.min)
+            act(vw(vp, 12, 14), run(7, 2))
+        if g1 in (5, 7):
+            for lv in (gl, g1):
+                for p0, c in blocks:
+                    dma("YS", ls, lambda T, lv=lv, c=c: T[lbn][16 * lv:16 * lv + 16, 2 * c:2 * c + 2],
+                        lambda T, lv=lv, p0=p0: T[vp][p0:p0 + 16, 2 * lv:2 * lv + 2],
+                        [vw(vp, 2 * lv, 2 * lv + 2, p0=p0, p1=p0 + 16)], [vw(lbn, 2 * c, 2 * c + 2, p0=16 * lv, p1=16 * lv + 16)], pri=(30 - 8 * s) if g1 == 7 else 20)
 
     for r in range(ROUNDS):
         last = r == ROUNDS - 1
@@ -328,12 +376,16 @@ def plan():
         remote(add, "as%d" % r, "al%d" % r, 2, "aa%d" % r)
         if last:
             for s in range(NS):
-                act(vw("bo%d" % s), vw("bw"), None, vw("lu%d" % s))
+                act(vw("bo%d" % s), vw("ix", 48, 96), None, vw("lu%d" % s))
                 dma("Y", "out", lambda T, s=s: T.bp[:, H * s:H * s + H], lambda T, s=s: T["bo%d" % s][0:128:16, :], [vw("bo%d" % s)], [])
         for s in range(NS):
             for t in range(4):
                 z = vw("zb%d" % s, t, 4 * H, 4)
-                tt(z, vw("nt", 48 * t, 48 * t + 48), vw("nf%d" % s, H * t, H * t + H), AO.subtract, ind=vw("lu%d" % s))
+                if t in ZS:
+                    act(vw("tg%d" % s, H * t, H * t + H), vw("nt", 48 * t, 48 * t + 48), None, vw("lu%d" % s))
+                    tt(z, vw("tg%d" % s, H * t, H * t + H), vw("ps%d" % (4 * s + t - 2), 0, H), AO.subtract)
+                else:
+                    tt(z, vw("nt", 48 * t, 48 * t + 48), vw("nf%d" % s, H * t, H * t + H), AO.subtract, ind=vw("lu%d" % s))
                 act(vw("zp", ZW * t + H * s, ZW * t + H * s + H), z, 64.0)
             quant(vw("zq%d" % s), vw("zs%d" % s), vw("zb%d" % s))
         for t in range(4):
@@ -369,14 +421,14 @@ def plan():
                         [vw("xs%d" % s)], [])
         add("", None, [vw("cq%d" % r), vw("cs%d" % r)], [vw("lq%d" % r, 0, 32), vw("ls%d" % r, 0, 32)], 0.0, sem="ac%d" % r, inc=2 * NE, lat=2.2, kind="a")
         tt(vw("tk"), vw("al%d" % r), vw("oc%d" % r), AO.is_gt)
-        tt(vw("tm"), vw("tk"), vw("dd"), AO.mult)
-        tt(vw("sr"), vw("tm"), vw("bs"), AO.add)
+        tt(vw("tm"), vw("tk"), vw("kc", 2, 4), AO.mult)
+        tt(vw("sr"), vw("tm"), vw("kc", 0, 2), AO.add)
         for t in range(4):
-            p = 4 + t if last else t
+            p = 4 + t if last else (2, 3, 6, 7)[t]
             mm(vw("ps%d" % p, 0, 128), vw("eq", 128 * t, 128 * t + 128), vw("es", 128 * t, 128 * t + 128), vw("lq%d" % r, 0, 128), vw("ls%d" % r, 0, 128))
             act(vw("tw%d" % r, 128 + 32 * t, 160 + 32 * t), vw("ps%d" % p, 0, 32))
         for c in range(2):
-            ts(vw("mo", 4 * c, 4 * c + 4), vw("k4"), vw("sr", c, c + 1), AO.add)
+            ts(vw("mo", 4 * c, 4 * c + 4), vw("kc", 4, 8), vw("sr", c, c + 1), AO.add)
             act(vw("tw%d" % (r + 1), c, 128, 2), vw("tw%d" % r), None, vw("mo", 4 * c, 4 * c + 4))
         for t in range(4):
             if last:
@@ -402,8 +454,16 @@ def remote(add, src, dst, n, sem):
     add("G", fn, [vw(src, 0, n)], [], 0.3, sem="loc", inc=NE, lat=0.0, kind="r", pri=6)
 
 
+def tag(o):
+    n = (o["W"] or o["R"])[0][0]
+    return (n[:-1] if n[-1].isdigit() else n) + ("d" if o["kind"] in "dr" else "")
+
+
 def schedule(ops):
     n = len(ops)
+    for o in ops:
+        o["pri"] += PRI.get(tag(o), 0.0)
+        o["bias"] = BIASES.get(tag(o), BIAS)
     deps = [set() for _ in range(n)]
     acc, groups = {}, {}
     for i, o in enumerate(ops):
@@ -453,7 +513,7 @@ def schedule(ops):
         for q, fn, dur in [(o["q"], o["fn"], o["dur"])] + ([o["alt"]] if "alt" in o else []):
             t = max(est[i], free.get(q, 0.0)) if q else est[i]
             r.append((t + dur, t, q, fn, dur))
-        return min(r, key=lambda x: x[0] + (BIAS if len(r) > 1 and x[2] == "V" else 0.0))
+        return min(r, key=lambda x: x[0] + (o["bias"] if len(r) > 1 and x[2] == "V" else 0.0))
     while est:
         W = {i: ways(i) for i in est}
         best = min(est, key=lambda i: (W[i][1], -pri[i] - ops[i]["pri"]))

from concourse.mybir import dt, AluOpType, ActivationFunctionType

ROUNDS = 3
H = 224
NS = 2
WIN = 2144
PEN0, ID0 = 1120, 1136
OCC = 32.0 * (PEN0 - 32)
ZW = 464
ZS = (3,)
NE = 8
COPY = ActivationFunctionType.Copy
AO = AluOpType

SCRATCH = {
    "ub": ("sbuf", [128, 512], "bfloat16"), "uq": ("sbuf", [128, 128], "float8_e4m3fn_x4"), "us": ("sbuf", [128, 128], "uint8"),
    "vb": ("sbuf", [128, 512], "bfloat16"), "vq": ("sbuf", [128, 128], "float8_e4m3fn_x4"), "vs": ("sbuf", [128, 128], "uint8"),
    "wq": ("sbuf", [128, 512], "float8_e4m3fn_x4"), "wp": ("sbuf", [128, 512], "uint8"),
    "ec": ("sbuf", [128, 2048], "bfloat16"), "em": ("sbuf", [128, 2048], "bfloat16"),
    "eq": ("sbuf", [128, 512], "float8_e4m3fn_x4"), "es": ("sbuf", [128, 512], "uint8"),
    "tb": ("sbuf", [128, 512], "bfloat16"), "tq": ("sbuf", [128, 128], "float8_e4m3fn_x4"), "tsc": ("sbuf", [128, 128], "uint8"),
    "zt": ("sbuf", [128, 512], "bfloat16"),
    "tii": ("sbuf", [128, 64], "int32"), "tif": ("sbuf", [128, 64], "bfloat16"), "td": ("dram", [16, 7168], "bfloat16"),
    "t0d": ("dram", [16, 1024], "int32"), "t0": ("sbuf", [128, WIN], "int32"), "tab": ("sbuf", [128, 7 * WIN], "bfloat16"),
    "rowi": ("sbuf", [128, 256], "int32"), "row": ("sbuf", [128, 256], "float32"), "flb": ("sbuf", [128, 256], "float32"),
    "idv": ("sbuf", [128, 32], "float32"), "pi": ("sbuf", [128, 1], "int32"), "pj": ("sbuf", [128, 1], "int32"),
    "k2": ("sbuf", [128, 2], "float32"), "ix": ("sbuf", [128, 96], "float32"),
    "d0": ("sbuf", [128, 96], "float32"), "dg": ("sbuf", [128, 96], "bfloat16"), "kc": ("sbuf", [128, 8], "float32"),
    "cf": ("sbuf", [128, 100], "bfloat16"), "ones": ("sbuf", [128, H], "bfloat16"), "oi": ("sbuf", [128, 2], "int32"),
    "nt": ("sbuf", [128, 192], "bfloat16"), "zp": ("sbuf", [128, 4 * ZW], "bfloat16"), "ct": ("sbuf", [128, 512], "bfloat16"),
    "na": ("sbuf", [128, 2], "float32"), "nn": ("sbuf", [128, 2], "float32"), "jo": ("sbuf", [128, 2], "uint16"),
    "thr": ("sbuf", [128, 2], "float32"), "tk": ("sbuf", [128, 2], "float32"), "tm": ("sbuf", [128, 2], "float32"),
    "sr": ("sbuf", [128, 2], "float32"), "mo": ("sbuf", [128, 8], "uint16"),
    "rto": ("sbuf", [128, 128], "float32"), "ys": ("sbuf", [128, 448], "float32"),
}
for _s in range(NS):
    for _n, _w, _d in (("xb", 4 * H, "bfloat16"), ("zb", 4 * H, "bfloat16"), ("nf", 4 * H, "bfloat16"), ("tg", 4 * H, "bfloat16"),
                       ("xq", H, "float8_e4m3fn_x4"), ("xs", H, "uint8"), ("zq", H, "float8_e4m3fn_x4"), ("zs", H, "uint8"),
                       ("bt", 100, "bfloat16"), ("sc", 100, "bfloat16"), ("go", 640, "bfloat16"), ("tr7", 8 * 320, "bfloat16"),
                       ("of", 40, "uint16"), ("va", 16, "bfloat16"), ("vp", 16, "bfloat16"), ("cb", 8, "bfloat16"),
                       ("lb", 16, "bfloat16"), ("lu", 14, "uint16"), ("qe", 2 * H, "bfloat16"), ("sn", 2 * H, "bfloat16"),
                       ("bo", H, "float32")):
        SCRATCH[_n + str(_s)] = ("sbuf", [128, _w], _d)
    SCRATCH["md" + str(_s)] = ("dram", [16, 7, 16], "bfloat16")
for _r in range(ROUNDS + 1):
    SCRATCH["oc%d" % _r] = ("sbuf", [128, 2], "float32")
    SCRATCH["tw%d" % _r] = ("sbuf", [128, 256], "bfloat16")
for _r in range(ROUNDS):
    SCRATCH["as%d" % _r] = ("sbuf", [128, 2], "float32")
    SCRATCH["al%d" % _r] = ("sbuf", [128, 2], "float32")
    SCRATCH["cq%d" % _r] = ("sbuf", [128, 128], "float8_e4m3fn_x4")
    SCRATCH["cs%d" % _r] = ("sbuf", [128, 128], "uint8")
    SCRATCH["lq%d" % _r] = ("sbuf", [128, 160], "float8_e4m3fn_x4")
    SCRATCH["ls%d" % _r] = ("sbuf", [128, 160], "uint8")
for _b in range(8):
    SCRATCH["ps%d" % _b] = ("psum", [128, 512], "float32")

DMA_SEMS = (["x0", "x1", "lu_", "lw", "lv", "ltr", "lti", "lfl", "lrow", "tdw", "t0d", "t0", "out"] + ["tb%d" % i for i in range(7)]
            + [k + "%d%d" % (s, r) for k in "lm" for s in range(NS) for r in range(ROUNDS)] + ["fr%d" % r for r in range(ROUNDS)])
SEMAPHORES = (["qV", "qS", "qT", "qG", "loc"] + ["d_" + n for n in DMA_SEMS]
              + ["aa%d" % r for r in range(ROUNDS)] + ["ac%d" % r for r in range(ROUNDS)])

CY = 0.00083
WAKE = 0.09
SLACK = 0.05
BIAS = 0.6
AHEAD = 5
PRI = {'go': 9.0, 'ps': 13.5, 'nn': 26.0, 'zb': 18.5, 'sn': 42.0, 'tw': -16.0, 'flb': 12.0, 'xq': 15.0, 'uq': 30.5, 'nt': -7.5, 'va': 26.0, 'rto': -18.0, 'bod': -6.0,
       'tq': 21.5, 'tm': 1.5, 'as': 5.0, 'xbd': -20.0, 'mdd': -14.5, 'ec': 12.5, 'ys': -8.5, 'cqd': 14.5, 'xqd': 2.5, 'tabd': 13.5, 'csd': 11.5, 'jo': -1.0,
       'vq': -14.5, 'ix': -14.0, 'sc': 5.5, 'mo': -40, 'cb': -16.5, 'rowid': -9.0, 'zt': 2.5, 'em': 5.5, 'tif': -10.5, 'tab': 1.5, 'row': -1.5, 'ones': -4.0,
       'thr': 8.0, 'wpd': -11.0, 'xsd': -59.5, 't': -9.5, 'na': 4.0, 'rtod': -3.0, 'oc': -6.5, 'sr': 8.0, 'vp': 2.0, 'pi': -15.0, 'tbd': 6.0, 'lbd': -16.5, 'asd': 5.0,
       'vbd': 24.5, 't0dd': 2.5, 'td': -1.0, 'idv': 13.5, 'qe': 0.5, 'tb': 1.5, 'cf': 33.5, 'lq': 13.0, 'rowd': 19.5, 'tdd': 7.5, 'tg': 0.5, 'tk': -6.0, 'd': -2.5,
       'oid': 19.5, 'dg': 28.5, 'lu': 3.0, 'ubd': -7.5, 'nf': -12.0, 'ocd': 11.5, 'tiid': -6.5, 'ysd': -3.0, 'bo': -8.0, 'pj': -1.0, 'wqd': 6.5, 'k': 2, 'bt': -1,
       'zp': -0.5, 'zq': 1, 'kc': -8.0, 'eq': -1, 'xb': 0.5, 'ct': 1}
BIASES = {'nf': 3, 'zp': 0.1, 'go': 3, 'qe': 0.1, 'tab': 0.4, 'tw': 0, 'ys': 0.1, 'nt': 0.2, 'rto': 0.1, 'bo': 0.2, 'vp': 0, 'tg': 0.4, 'ct': 3}


def vw(name, c0=0, c1=None, st=1, p0=0, p1=128, ps=1):
    if c1 is None:
        c1 = SCRATCH[name][1][1]
    return (name, c0, c1, st, p0, p1, ps)


def width(a):
    return len(range(a[1], a[2], a[3]))


def AP(T, a):
    n, c0, c1, st, p0, p1, ps = a
    rows = slice(p0, p1) if ps == 1 else slice(p0, p1, ps)
    cols = slice(c0, c1) if st == 1 else slice(c0, c1, st)
    return T[n][rows, cols]


def overlap(a, b):
    if a[0][:2] == "ps" and a[0] == b[0]:
        return True
    if a[1] >= b[2] or b[1] >= a[2] or a[4] >= b[5] or b[4] >= a[5]:
        return False
    if a[3] == b[3] and a[3] > 1 and (a[1] - b[1]) % a[3]:
        return False
    return True


def plan():
    ops = []

    def add(q, fn, R, W, dur, sem=None, inc=1, lat=0.0, pri=0.0, kind="c"):
        ops.append({"q": q, "fn": fn, "R": R, "W": W, "dur": dur, "sem": sem or "q" + q, "inc": inc, "lat": lat, "pri": pri, "kind": kind})

    def two(*v):
        return all(SCRATCH[a[0]][2] in ("bfloat16", "uint16") for a in v)

    def memset(o, val):
        add("V", lambda T, g, o=o, val=val: g.vector.memset(AP(T, o), val), [], [o], 0.055 + width(o) * CY * (0.5 if two(o) else 1))

    def tt(o, a, b, op, ind=None, pri=0.0):
        def fn(T, g):
            i0 = AP(T, a)
            if ind is not None:
                i0 = i0.indirect(AP(T, ind))
            return g.vector.tensor_tensor(AP(T, o), i0, AP(T, b), op)
        f = 1.56 if ind is not None else (1.0 if "ps" in (a[0][:2], b[0][:2]) else 2.0)
        add("V", fn, [a, b] + ([ind] if ind is not None else []), [o], 0.055 + width(o) * CY * f, pri=pri)

    def ts(o, a, s1, op0, s2=None, op1=None, pri=0.0):
        def fn(T, g):
            x1 = AP(T, s1) if isinstance(s1, tuple) else s1
            x2 = AP(T, s2) if isinstance(s2, tuple) else s2
            if op1 is None:
                return g.vector.tensor_scalar(AP(T, o), AP(T, a), x1, None, op0)
            return g.vector.tensor_scalar(AP(T, o), AP(T, a), x1, x2, op0, op1)
        add("V", fn, [a] + [s for s in (s1, s2) if isinstance(s, tuple)], [o], 0.055 + width(o) * CY, pri=pri)

    def vcopy(o, a):
        add("V", lambda T, g: g.vector.tensor_copy(AP(T, o), AP(T, a)), [a], [o], 0.055 + width(o) * CY)

    def scan(o, a, b, init, op0, op1, pri=0.0):
        add("V", lambda T, g: g.vector.tensor_tensor_scan(AP(T, o), AP(T, a), AP(T, b), init, op0, op1), [a, b], [o], 0.055 + width(o) * CY * 0.5, pri=pri)

    def flip(o, a):
        add("V", lambda T, g: g.vector.transpose(AP(T, o), AP(T, a)), [a], [o], 0.055 + width(o) * CY * 0.5)

    def quant(o, s, a):
        add("V", lambda T, g: g.vector.quantize_mx(AP(T, o), AP(T, s), AP(T, a)), [a], [o, s], 0.02 + width(a) * 0.00022)

    def act(o, a, scale=None, ind=None, pri=0.0):
        def src(T):
            i = AP(T, a)
            return i if ind is None else i.indirect(AP(T, ind))

        def fs(T, g):
            if scale is None:
                return g.scalar.activation(AP(T, o), src(T), COPY)
            return g.scalar.activation(AP(T, o), src(T), COPY, scale=scale)

        def fv(T, g):
            if scale is None:
                return g.vector.tensor_copy(AP(T, o), src(T))
            return g.vector.tensor_scalar(AP(T, o), src(T), scale, None, AO.mult)
        f = 1.56 if ind is not None else 1.0
        add("S", fs, [a] + ([ind] if ind is not None else []), [o], 0.065 + width(o) * CY * f, pri=pri)
        ops[-1]["alt"] = ("V", fv, 0.055 + width(o) * CY * (0.5 if ind is None and two(a, o) else f))

    def mm(o, l, ls, m, ms):
        add("T", lambda T, g: g.tensor.matmul_mx(AP(T, o), AP(T, l), AP(T, ls), AP(T, m), AP(T, ms), True, True),
            [l, ls, m, ms], [o], 0.03 + (width(m) + 16) * 0.00075)

    def dma(q, sem, o, i, R, W, size=0, pri=0.0):
        fy = lambda T, g: g.sync.dma_start(o(T), i(T))
        fs = lambda T, g: g.scalar.dma_start(o(T), i(T))
        add(q[0], fy if q[0] == "Y" else fs, R, W, 0.07, sem="d_" + sem, inc=16, lat=1.9 + size / 200000.0, pri=pri, kind="d")
        if q == "YS":
            ops[-1]["alt"] = ("S", fs, 0.07)

    for s in range(NS):
        dma("Y", "x%d" % s, lambda T, s=s: T["xb%d" % s][:], lambda T, s=s: T.x[:, 4 * H * s:4 * H * (s + 1)], [], [vw("xb%d" % s)], 230000, pri=50)
    dma("S", "lti", lambda T: T.tii[0:112, :], lambda T: T.ti[:], [], [vw("tii", p1=112)], 28000, pri=60)
    for gl in range(8):
        dma("S", "lu_", lambda T, gl=gl: T.ub[:, 20 * gl:20 * gl + 20], lambda T, gl=gl: T.u[:, 64 * gl:64 * gl + 20], [], [vw("ub", 20 * gl, 20 * gl + 20)], 10000, pri=50)
    dma("S", "lu_", lambda T: T.ub[:, 160:512], lambda T: T.u[:, 0:352], [], [vw("ub", 160, 512)], 90000, pri=50)
    dma("S", "lrow", lambda T: T.rowi[0:1, :], lambda T: T.fl[:], [], [vw("rowi", p1=1)], pri=45)
    dma("S", "lfl", lambda T: T.oi[:], lambda T: T.fl[:], [], [vw("oi")], pri=10)
    dma("Y", "ltr", lambda T: T.tb[:, 0:128], lambda T: T.tr[:], [], [vw("tb", 0, 128)], 30000, pri=30)
    ts(vw("tif", p1=112), vw("tii", p1=112), 32.0, AO.mult, 32.0, AO.add, pri=60)
    for m in range(16):
        dma("YS"[m % 2], "tdw", lambda T, m=m: T.td[m:m + 1, :], lambda T: T.tif[0:112, :], [vw("tif", p1=112)], [("td", 0, 7168, 1, m, m + 1, 1)], 14000, pri=55)
    for m in range(8):
        dma("YS"[m % 2], "t0d", lambda T, m=m: T.t0d[m:m + 1, :], lambda T: T.ti[0:1, :], [], [("t0d", 0, 1024, 1, m, m + 1, 1)], 4000, pri=70)
    for m in range(16):
        dma("YS"[m % 2], "t0", lambda T, m=m: T.t0[8 * m:8 * m + 8, 0:1024], lambda T: T.t0d[0:8, :], [("t0d", 0, 1024, 1, 0, 8, 1)], [vw("t0", 0, 1024, p0=8 * m, p1=8 * m + 8)], 32000, pri=65)
    for gl in (1, 2, 3, 4, 5, 6, 0):
        o = WIN * gl
        a = o + (0 if gl == 0 else 33)
        if gl:
            memset(vw("tab", o, a), 0.0)
        if gl in (4, 6):
            memset(vw("tab", o + ID0 - 32, o + ID0 - 31), 0.0)
        if gl == 3:
            memset(vw("tab", o + PEN0 - 32, o + PEN0 - 31), 0.0)
        for m in range(8):
            dma("YS"[m % 2] if gl in (1, 2, 3) else "Y", "tb%d" % gl, lambda T, m=m, a=a: T.tab[16 * m:16 * m + 16, a:a + 1024], lambda T, gl=gl: T.td[:, 1024 * gl:1024 * gl + 1024],
                [("td", 1024 * gl, 1024 * gl + 1024, 1, 0, 16, 1)], [vw("tab", a - a % 8, a + 1024 + (-a) % 8, p0=16 * m, p1=16 * m + 16)], 32000, pri=40 - 2 * (gl or 7))
    dma("Y", "lw", lambda T: T.wq[:].bitcast(dt.uint8), lambda T: T.wc[:], [], [vw("wq")], 260000)
    dma("Y", "lw", lambda T: T.wp[:], lambda T: T.ws[:], [], [vw("wp")], 65000)
    dma("Y", "lv", lambda T: T.vb[:], lambda T: T.v[:], [], [vw("vb")], 130000, pri=-20)

    def iota(o, pat, base, cm, flag):
        def fn(T, g):
            if flag:
                return g.iota(AP(T, o), pat, base, cm, allow_small_or_imprecise_dtypes=True)
            return g.iota(AP(T, o), pat, base, cm)
        add("G", fn, [], [o], 0.13 + 2 * width(o) * CY)
    memset(vw("em"), -0.015625)
    for h in range(2):
        v = vw("ec", 1024 * h, 1024 * h + 1024)
        iv = vw("em", 1024 * h, 1024 * h + 1024)
        add("G", lambda T, g, v=v, iv=iv, h=h: g.affine_select(AP(T, v), AP(T, iv), [[-1, 2], [1, 512]], AO.is_equal, 0.0, -2 * h, -4), [iv], [v], 0.17 + 2048 * CY)
        quant(vw("eq", 256 * h, 256 * h + 256), vw("es", 256 * h, 256 * h + 256), v)
    iota(vw("idv"), [[32, 32]], 32, 0, True)
    iota(vw("pi"), [[0, 1]], 0, 1, False)
    iota(vw("ix", 0, 48), [[1, 48]], 0, 0, True)
    iota(vw("ix", 48, 96), [[1, 48]], -1, 0, True)
    iota(vw("kc", 4, 8), [[32, 4]], 0, 0, True)
    ts(vw("pj"), vw("pi"), 15, AO.bitwise_and)
    for c in range(2):
        ts(vw("k2", c, c + 1), vw("pj"), 2.0, AO.mult, 1.0 + c, AO.add)
        ts(vw("d0", 48 * c, 48 * c + 48), vw("ix", 0, 48), vw("k2", c, c + 1), AO.not_equal, -448.0, AO.mult)
        ts(vw("kc", c, c + 1), vw("pj"), 2.0, AO.mult, float(c), AO.add)
        ts(vw("kc", 2 + c, 3 + c), vw("pj"), -1.0, AO.mult, 128.0 + 15 * c, AO.add)
    ts(vw("dg"), vw("d0"), -224.0, AO.add)
    memset(vw("cf"), 2.0)
    memset(vw("cf", 0, 100, 5), 0.0)
    for s in range(NS):
        memset(vw("cf", 50 * s + 40, 50 * s + 50), 0.0)
        for b in range(2):
            memset(vw("bt%d" % s, 50 * b + 40, 50 * b + 50), 32.0 * ID0)
        for gl in (4, 6):
            c = 320 * gl + 32 * (9 - gl)
            memset(vw("tr7%d" % s, c, c + 32), 32.0 * (ID0 - 32))
    memset(vw("ones"), 1.0)
    memset(vw("nt"), 0.0)
    for t in range(4):
        memset(vw("zp", ZW * t + 448, ZW * t + ZW), 0.0)
    memset(vw("tb", 128, 512), 0.0)
    memset(vw("zt"), 0.0)
    memset(vw("ct"), 0.0)
    for gl in (0, 1, 2, 4, 6):
        act(vw("tab", WIN * gl + ID0, WIN * gl + ID0 + 993, 32), vw("idv"))
    for r in range(ROUNDS):
        quant(vw("lq%d" % r, 32, 160), vw("ls%d" % r, 32, 160), vw("zt"))
    quant(vw("uq"), vw("us"), vw("ub"))
    vcopy(vw("row", p1=1), vw("rowi", p1=1))
    vcopy(vw("oc0"), vw("oi"))

    def flags_out():
        for a, b in ((0, 96), (96, 224)):
            add("G", lambda T, g, a=a, b=b: g.partition_broadcast(T.flb[:, a:b], T.row[0:1, a:b], 128), [vw("row", a, b, p1=1)], [vw("flb", a, b)], 0.14 + 4 * (b - a) * CY, pri=10)
        for gl, at in ((0, 2 * WIN + 4), (1, 2 * WIN + 8), (2, 2 * WIN), (3, 3 * WIN), (4, 4 * WIN), (5, 5 * WIN), (6, 6 * WIN)):
            act(vw("tab", at + PEN0, at + PEN0 + 993, 32), vw("flb", 32 * gl, 32 * gl + 32), OCC)
    flags_out()
    ts(vw("t0", ID0, ID0 + 993, 32), vw("idv"), 0.03125, AO.mult, -1.0, AO.add)

    def scores(s):
        for b in range(2):
            p = vw("ps%d" % (4 * s + b), 0, 128)
            mm(p, vw("xq%d" % s, 96 * b, 96 * b + 128), vw("xs%d" % s, 96 * b, 96 * b + 128), vw("uq"), vw("us"))
            ts(vw("bt%d" % s, 50 * b, 50 * b + 40), vw("ps%d" % (4 * s + b), 0, 40), 0.0, AO.is_gt, 32.0, AO.mult)
        scan(vw("sc%d" % s), vw("cf"), vw("bt%d" % s), 0.0, AO.mult, AO.add)

    def unpack(s):
        for t in range(4):
            p = vw("ps%d" % (4 * s + (2, 3, 0, 1)[t]), 0, H)
            mm(p, vw("eq", 128 * t, 128 * t + 128), vw("es", 128 * t, 128 * t + 128), vw("xq%d" % s), vw("xs%d" % s))
            if t not in ZS:
                act(vw("nf%d" % s, H * t, H * t + H), p)

    for s in range(NS):
        quant(vw("xq%d" % s), vw("xs%d" % s), vw("xb%d" % s))
        scores(s)
    for s in range(NS):
        unpack(s)
    quant(vw("tq"), vw("tsc"), vw("tb"))
    for t in range(4):
        pb = (2, 3, 6, 7)[t]
        mm(vw("ps%d" % pb, 0, 128), vw("eq", 128 * t, 128 * t + 128), vw("es", 128 * t, 128 * t + 128), vw("tq"), vw("tsc"))
        act(vw("tw0", 32 * t, 32 * t + 32), vw("ps%d" % pb, 0, 32))
        act(vw("nt", 48 * t + 1, 48 * t + 33), vw("tw0", 32 * t, 32 * t + 32))
    quant(vw("vq"), vw("vs"), vw("vb"))

    def level(s, gl, r):
        tr, va, vp, of, go, cb = ["%s%d" % (n, s) for n in ("tr7", "va", "vp", "of", "go", "cb")]
        fo, fg, base = 20 * (gl % 2), 320 * (gl % 2), 320 * gl

        def run(lv, k):
            return vw(tr, 320 * lv + 32 * k, 320 * lv + 32 * k + 17, 16)
        pre = 3 if gl == 2 else 0
        nin = 7 - gl + (1, 0, 0, 0, 2, 1, 2)[gl]
        pv = 4 if gl == 3 else 1
        for k in range(2):
            if gl == 0:
                i0, b = vw("sc%d" % s, 50 * k + 9, 50 * k + 45, 5), vw("sc%d" % s, 50 * k + 4, 50 * k + 5)
            else:
                i0 = vw(tr, base + 32 * pv + 16 * k, base + 32 * (pv + nin - 1) + 16 * k + 1, 32)
                b = vw(tr, base + 16 * k, base + 16 * k + 1) if gl < 3 else vw(va if gl in (4, 6) else vp, 2 * gl + k, 2 * gl + k + 1)
            ts(vw(of, fo + 2 * pre + k, fo + 2 * (pre + nin) - 1 + k, 2), i0, 0.03125, AO.mult, b, AO.add)
        runs = pre + nin
        if gl in (1, 2, 3):
            ts(vw(of, fo + 2 * runs, fo + 2 * runs + 2), vw(vp, 6, 8) if gl == 3 else run(gl, 0), float((PEN0 if gl == 3 else ID0) - 32), AO.add)
            runs += 1
        if gl == 2:
            ts(vw(of, fo, fo + 2), vw("sc%d" % s, 4, 55, 50), float(PEN0 + 4), AO.add)
            ts(vw(of, fo + 2, fo + 4), run(2, 6), float(PEN0 + 8 - 32), AO.add)
            ts(vw(of, fo + 4, fo + 6), run(2, 0), float(PEN0 - 32), AO.add)
        if gl == 0 and r == 0:
            add("V", lambda T, g: g.vector.tensor_scalar(T[go][:, 0:256], T.t0[:].indirect(T[of][:, 0:16]), 32.0, 32.0, AO.mult, AO.add),
                [vw("t0"), vw(of, 0, 16)], [vw(go, 0, 256)], 0.055 + 256 * CY * 1.56)
        else:
            act(vw(go, fg, fg + 32 * runs), vw("tab", WIN * gl, WIN * gl + WIN), None, vw(of, fo, fo + 2 * runs))
        n = base + 320
        flip(vw(tr, n, n + 32 * runs), vw(go, fg, fg + 32 * runs))
        g1 = gl + 1
        blocks = [(32 * a, a) for a in range(4)] + [(32 * a + 16, a + 3) for a in range(1, 4)]
        lbn, ls, md = "lb%d" % s, "l%d%d" % (s, r), "md%d" % s
        if g1 == 1:
            act(vw(vp, 0, 2), run(1, 7))
        if g1 == 3:
            for k in range(2):
                v = vw(tr, n + 16 * k, n + 97 + 16 * k, 32)
                scan(vw(cb, k, 7 + k, 2), v, v, 100000.0, AO.min, AO.min)
            for lv, v, c in ((3, run(3, 3), 6), (1, run(1, 0), 0), (2, run(3, 8), 2)):
                tt(vw(vp, 2 * lv, 2 * lv + 2), v, vw(cb, c, c + 2), AO.min)
            for p0, c in blocks:
                dma("YS", "m%d%d" % (s, r), lambda T, c=c: T[md][:, c, 0:8], lambda T, p0=p0: T[vp][p0:p0 + 16, 0:8],
                    [vw(vp, 0, 8, p0=p0, p1=p0 + 16)], [(md, 16 * c, 16 * c + 16, 1, 0, 16, 1)], pri=10)
            for lv in range(4):
                dma("Y", ls, lambda T, lv=lv: T[lbn][16 * lv:16 * lv + 16, 0:14], lambda T, lv=lv: T[md][:, :, 2 * lv:2 * lv + 2],
                    [(md, 0, 112, 1, 0, 16, 1)], [vw(lbn, 0, 14, p0=16 * lv, p1=16 * lv + 16)], pri=10)
        if g1 == 4:
            tt(vw(va, 8, 10), run(4, 0), run(4, 4), AO.min)
        if g1 == 5:
            tt(vw(vp, 10, 12), run(5, 0), run(5, 3), AO.min)
            act(vw(vp, 8, 10), run(5, 4))
        if g1 == 6:
            tt(vw(va, 12, 14), run(6, 0), run(6, 2), AO.min)
        if g1 == 7:
            tt(vw(vp, 14, 16), run(7, 0), run(7, 1), AO.min)
            act(vw(vp, 12, 14), run(7, 2))
        if g1 in (5, 7):
            for lv in (gl, g1):
                for p0, c in blocks:
                    dma("YS", ls, lambda T, lv=lv, c=c: T[lbn][16 * lv:16 * lv + 16, 2 * c:2 * c + 2],
                        lambda T, lv=lv, p0=p0: T[vp][p0:p0 + 16, 2 * lv:2 * lv + 2],
                        [vw(vp, 2 * lv, 2 * lv + 2, p0=p0, p1=p0 + 16)], [vw(lbn, 2 * c, 2 * c + 2, p0=16 * lv, p1=16 * lv + 16)], pri=(30 - 8 * s) if g1 == 7 else 20)

    for r in range(ROUNDS):
        last = r == ROUNDS - 1
        for gl in range(7):
            for s in range(NS):
                n0 = len(ops)
                level(s, gl, r)
                for o in ops[n0:]:
                    o["pri"] += AHEAD * (1 - s)
        for s in range(NS):
            lu = vw("lu%d" % s)
            ts(lu, vw("lb%d" % s, 0, 14), 0.03125, AO.mult, pri=3)
            for c in range(2):
                e = vw("qe%d" % s, H * c, H * c + H)
                act(e, vw("dg", 48 * c, 48 * c + 48), None, lu, pri=6)
                scan(vw("sn%d" % s, H * c, H * c + H), e, vw("ones"), -672.0, AO.max, AO.add, pri=6)
        ts(vw("thr"), vw("oc%d" % r), 1224.0, AO.mult, -224.0, AO.add)
        ts(vw("na"), vw("sn0", H - 1, 2 * H, H), 224.0, AO.add, pri=6)
        tt(vw("nn"), vw("na"), vw("sn1", H - 1, 2 * H, H), AO.max, pri=6)
        tt(vw("as%d" % r), vw("nn"), vw("thr"), AO.is_gt, pri=6)
        ts(vw("jo"), vw("nn"), -1.0, AO.mult, 224.0, AO.add, pri=3)
        remote(add, "as%d" % r, "al%d" % r, 2, "aa%d" % r)
        if last:
            for s in range(NS):
                act(vw("bo%d" % s), vw("ix", 48, 96), None, vw("lu%d" % s))
                dma("Y", "out", lambda T, s=s: T.bp[:, H * s:H * s + H], lambda T, s=s: T["bo%d" % s][0:128:16, :], [vw("bo%d" % s)], [])
        for s in range(NS):
            for t in range(4):
                z = vw("zb%d" % s, t, 4 * H, 4)
                if t in ZS:
                    act(vw("tg%d" % s, H * t, H * t + H), vw("nt", 48 * t, 48 * t + 48), None, vw("lu%d" % s))
                    tt(z, vw("tg%d" % s, H * t, H * t + H), vw("ps%d" % (4 * s + t - 2), 0, H), AO.subtract)
                else:
                    tt(z, vw("nt", 48 * t, 48 * t + 48), vw("nf%d" % s, H * t, H * t + H), AO.subtract, ind=vw("lu%d" % s))
                act(vw("zp", ZW * t + H * s, ZW * t + H * s + H), z, 64.0)
            quant(vw("zq%d" % s), vw("zs%d" % s), vw("zb%d" % s))
        for t in range(4):
            act(vw("ct", t, 128, 4), vw("zp", ZW * t, ZW * t + ZW), None, vw("jo"), pri=1)
        quant(vw("cq%d" % r), vw("cs%d" % r), vw("ct"))
        remote(add, "cq%d" % r, "lq%d" % r, 32, "ac%d" % r)
        remote(add, "cs%d" % r, "ls%d" % r, 32, "ac%d" % r)
        for s in range(NS):
            for k in range(4):
                p = vw("ps%d" % (4 * s + k), 0, H)
                mm(p, vw("wq", 128 * k, 128 * k + 128), vw("wp", 128 * k, 128 * k + 128), vw("zq%d" % s), vw("zs%d" % s))
                tt(vw("xb%d" % s, k, 4 * H, 4), p, vw("zp", ZW * k + H * s, ZW * k + H * s + H), AO.add)
            quant(vw("xq%d" % s), vw("xs%d" % s), vw("xb%d" % s))
            if not last:
                scores(s)
        add("", None, [vw("as%d" % r)], [vw("al%d" % r)], 0.0, sem="aa%d" % r, inc=NE, lat=1.8, kind="a")
        tt(vw("oc%d" % (r + 1)), vw("oc%d" % r), vw("al%d" % r), AO.max, pri=6)
        dma("Y", "fr%d" % r, (lambda T: T.bp[:, 448:480]) if last else (lambda T: T.row[0:1, :]), lambda T, r=r: T["oc%d" % (r + 1)][:],
            [vw("oc%d" % (r + 1))], [] if last else [vw("row", p1=1)], pri=6)
        if not last:
            flags_out()
            for s in range(NS):
                unpack(s)
        else:
            for s in range(NS):
                p = vw("ps%d" % (4 * s), 0, H)
                mm(p, vw("vq"), vw("vs"), vw("xq%d" % s), vw("xs%d" % s))
                act(vw("ys", H * s, H * s + H), p)
                dma("Y", "out", lambda T, s=s: T.y[:, H * s:H * s + H], lambda T, s=s: T.ys[:, H * s:H * s + H], [vw("ys", H * s, H * s + H)], [], 115000)
                dma("Y", "out", lambda T, s=s: T.oc[:, 4 * H * s:4 * H * (s + 1)], lambda T, s=s: T["xq%d" % s][:].bitcast(dt.uint8), [vw("xq%d" % s)], [], 115000)
                for k in range(4):
                    dma("Y", "out", lambda T, s=s, k=k: T.osc[4 * k:4 * k + 4, H * s:H * s + H], lambda T, s=s, k=k: T["xs%d" % s][32 * k:32 * k + 4, :],
                        [vw("xs%d" % s)], [])
        add("", None, [vw("cq%d" % r), vw("cs%d" % r)], [vw("lq%d" % r, 0, 32), vw("ls%d" % r, 0, 32)], 0.0, sem="ac%d" % r, inc=2 * NE, lat=2.2, kind="a")
        tt(vw("tk"), vw("al%d" % r), vw("oc%d" % r), AO.is_gt)
        tt(vw("tm"), vw("tk"), vw("kc", 2, 4), AO.mult)
        tt(vw("sr"), vw("tm"), vw("kc", 0, 2), AO.add)
        for t in range(4):
            p = 4 + t if last else (2, 3, 6, 7)[t]
            mm(vw("ps%d" % p, 0, 128), vw("eq", 128 * t, 128 * t + 128), vw("es", 128 * t, 128 * t + 128), vw("lq%d" % r, 0, 128), vw("ls%d" % r, 0, 128))
            act(vw("tw%d" % r, 128 + 32 * t, 160 + 32 * t), vw("ps%d" % p, 0, 32))
        for c in range(2):
            ts(vw("mo", 4 * c, 4 * c + 4), vw("kc", 4, 8), vw("sr", c, c + 1), AO.add)
            act(vw("tw%d" % (r + 1), c, 128, 2), vw("tw%d" % r), None, vw("mo", 4 * c, 4 * c + 4))
        for t in range(4):
            if last:
                act(vw("rto", t, 128, 4), vw("tw%d" % (r + 1), 32 * t, 32 * t + 32), -64.0)
            else:
                act(vw("nt", 48 * t + 1, 48 * t + 33), vw("tw%d" % (r + 1), 32 * t, 32 * t + 32))
    dma("Y", "out", lambda T: T.rt[:], lambda T: T.rto[:], [vw("rto")], [], 65000)
    return ops


def remote(add, src, dst, n, sem):
    code = SCRATCH[src][2].startswith("float8")

    def fn(T, g, topo, core, to):
        a, b = T[dst][:, 0:n], T[src][:, 0:n]
        if code:
            a, b = a.bitcast(dt.uint8), b.bitcast(dt.uint8)
        rid, pid = topo.addr(to)[0], topo.addr(to)[1]
        m = 0
        for e in topo.engines(core, to)[:NE]:
            m |= 1 << e
        return g.remote_dma(a, b, T.sem[sem], T.sem.loc, pid, rid, m)
    add("G", fn, [vw(src, 0, n)], [], 0.3, sem="loc", inc=NE, lat=0.0, kind="r", pri=6)


def tag(o):
    n = (o["W"] or o["R"])[0][0]
    return (n[:-1] if n[-1].isdigit() else n) + ("d" if o["kind"] in "dr" else "")


def schedule(ops):
    n = len(ops)
    for o in ops:
        o["pri"] += PRI.get(tag(o), 0.0)
        o["bias"] = BIASES.get(tag(o), BIAS)
    deps = [set() for _ in range(n)]
    acc, groups = {}, {}
    for i, o in enumerate(ops):
        if o["kind"] == "d":
            groups.setdefault(o["sem"], []).append(i)
    for i, o in enumerate(ops):
        for v, w in [(a, False) for a in o["R"]] + [(a, True) for a in o["W"]]:
            for j, u, uw in acc.setdefault(v[0], []):
                if j == i or j in deps[i]:
                    continue
                bank = v[0][:2] == "ps" and (ops[j]["q"] != o["q"] or "alt" in o or "alt" in ops[j])
                if (w or uw or bank) and overlap(u, v):
                    deps[i].add(j)
        for v, w in [(a, False) for a in o["R"]] + [(a, True) for a in o["W"]]:
            lst = acc[v[0]]
            if w:
                lst[:] = [t for t in lst if not (v[3] == 1 and v[6] == 1 and t[1][1] >= v[1] and t[1][2] <= v[2] and t[1][4] >= v[4] and t[1][5] <= v[5]) or t[0] == i]
            lst.append((i, v, w))
    for i in range(n):
        for j in list(deps[i]):
            if ops[j]["kind"] == "d":
                for m in groups[ops[j]["sem"]]:
                    assert m < i
                    deps[i].add(m)
    for i, o in enumerate(ops):
        if o["kind"] == "a":
            for j in range(i):
                if ops[j]["kind"] == "r" and any(a[0] == b[0] for a in ops[j]["R"] for b in o["R"]):
                    deps[i].add(j)
    succ = [[] for _ in range(n)]
    for i in range(n):
        for j in deps[i]:
            succ[j].append(i)
    pri = [0.0] * n
    for i in range(n - 1, -1, -1):
        o = ops[i]
        pri[i] = o["dur"] + o["lat"] + max([pri[k] + WAKE for k in succ[i]], default=0.0)
    left = [len(d) for d in deps]
    done, free, order, est = [0.0] * n, {}, [], {}
    for i in range(n):
        if not left[i]:
            est[i] = 0.0

    def ways(i):
        o = ops[i]
        r = []
        for q, fn, dur in [(o["q"], o["fn"], o["dur"])] + ([o["alt"]] if "alt" in o else []):
            t = max(est[i], free.get(q, 0.0)) if q else est[i]
            r.append((t + dur, t, q, fn, dur))
        return min(r, key=lambda x: x[0] + (o["bias"] if len(r) > 1 and x[2] == "V" else 0.0))
    while est:
        W = {i: ways(i) for i in est}
        best = min(est, key=lambda i: (W[i][1], -pri[i] - ops[i]["pri"]))
        t0 = W[best][1]
        cand = [i for i in est if W[i][2] == W[best][2] and W[i][1] <= t0 + SLACK]
        i = max(cand, key=lambda i: (pri[i] + ops[i]["pri"], -i))
        end, t, q, fn, dur = W[i]
        if "alt" in ops[i]:
            ops[i].update({"q": q, "fn": fn, "dur": dur})
            if ops[i]["kind"] == "c":
                ops[i]["sem"] = "q" + q
        if q:
            free[q] = end
        done[i] = end + ops[i]["lat"]
        order.append((t, i))
        del est[i]
        for k in succ[i]:
            left[k] -= 1
            if not left[k]:
                est[k] = max(done[j] for j in deps[k]) + WAKE
    return [i for _, i in order], deps, done, order


_CACHE = {}


def rank_program(g, core, T, topo):
    rank = T.rank_of(core)
    if rank is None:
        return
    if not _CACHE:
        _CACHE["ops"] = plan()
        _CACHE["order"] = schedule(_CACHE["ops"])
    ops = _CACHE["ops"]
    order, deps, _, _ = _CACHE["order"]
    to = T.cores[(rank + 1) % len(T.cores)]
    queue = {"V": g.vector, "S": g.scalar, "T": g.tensor, "G": g, "Y": g.sync}
    total, count, known, clock = {}, {}, {}, {}
    for o in ops:
        if o["kind"] == "d":
            total[o["sem"]] = total.get(o["sem"], 0) + o["inc"]

    def need(j):
        o = ops[j]
        return (o["sem"], total[o["sem"]] if o["kind"] == "d" else o["inc"] if o["kind"] == "a" else count[j])

    for i in order:
        o = ops[i]
        q = o["q"]
        if o["kind"] == "a":
            clock[i] = {o["sem"]: o["inc"]}
            continue
        k = known.setdefault(q, {})
        want = {}
        for j in sorted(deps[i], reverse=True):
            sem, c = need(j)
            if k.get(sem, 0) < c and want.get(sem, (0, 0))[0] < c:
                want[sem] = (c, j)
        for sem in sorted(want, key=lambda s: -want[s][1]):
            c, j = want[sem]
            if k.get(sem, 0) >= c:
                continue
            queue[q].wait_ge(T.sem[sem], c)
            for s2, c2 in clock[j].items():
                if k.get(s2, 0) < c2:
                    k[s2] = c2
            if k.get(sem, 0) < c:
                k[sem] = c
        if o["kind"] == "r":
            o["fn"](T, g, topo, core, to)
            total["loc"] = total.get("loc", 0) + o["inc"]
            clock[i] = {}
            continue
        o["fn"](T, g).then_inc(T.sem[o["sem"]], o["inc"])
        clock[i] = dict(k)
        if o["kind"] == "d":
            clock[i][o["sem"]] = total[o["sem"]]
        else:
            total[o["sem"]] = total.get(o["sem"], 0) + 1
            count[i] = total[o["sem"]]
            clock[i][o["sem"]] = count[i]
    for r in range(ROUNDS):
        g.wait_ge(T.sem["aa%d" % r], NE)
        g.wait_ge(T.sem["ac%d" % r], 2 * NE)
    for sem in total:
        g.wait_ge(T.sem[sem], total[sem])
